import numpy as np
import ml_dtypes


def mxq(x, axis, fmt="e4m3"):
    dtype, down = {"e4m3": (ml_dtypes.float8_e4m3fn, 7), "e5m2": (ml_dtypes.float8_e5m2, 14)}[fmt]
    v = np.moveaxis(np.asarray(x, np.float32).astype(ml_dtypes.bfloat16).astype(np.float64), axis, -1)
    blocks = v.reshape(v.shape[:-1] + (-1, 32))
    amax = np.abs(blocks).max(-1, keepdims=True)
    byte = np.maximum(np.where(amax > 0, np.frexp(amax)[1] - 1 + 127, 0) - down, 1)
    scale = np.exp2(byte - 127.0)
    codes = (blocks / scale).astype(np.float32).astype(dtype).astype(np.float64)
    return np.moveaxis((codes * scale).reshape(v.shape), -1, axis)


WIDE = False


def mx_kscale(k):
    if not WIDE:
        return np.ones(k)
    levels = np.array([10, -10, 5, -5, 0])
    if k % 512:
        return np.exp2(np.random.permutation(np.resize(levels, k // 32))).repeat(32)
    a = np.empty((k // 512, 16))
    for p in range(k // 512):
        a[p, :8] = np.random.permutation(np.resize(levels, 8))
        for g in range(8):
            far = levels[np.abs(levels - a[p, g]) >= 10]
            a[p, g + 8] = far[np.random.randint(len(far))]
    return np.exp2(a.ravel()).repeat(32)


def f64(x):
    return np.asarray(x).astype(np.float64)


def striped(idx):
    return np.tile(idx.reshape(-1, 16).T, (8, 1)).astype(np.uint16)


def unstriped(offs):
    return offs[:16].T.reshape(-1).astype(np.int64)


E2M1 = np.array([0.0, 0.5, 1.0, 1.5, 2.0, 3.0, 4.0, 6.0, -0.0, -0.5, -1.0, -1.5, -2.0, -3.0, -4.0, -6.0])


def pack_weight(w, fmt):
    k, n = w.shape
    w = f64(np.asarray(w, np.float32).astype(ml_dtypes.bfloat16)).reshape(k // 32, 32, n)
    amax = np.abs(w).max(1)
    if fmt == "e4m3":
        byte = np.frexp(amax)[1] - 1 + 127 - 7
    else:
        mant, ex = np.frexp(amax / 6.0)
        byte = np.where(mant > 0.5, ex, ex - 1) + 127
    byte = np.clip(np.where(amax > 0, byte, 1), 1, 254)
    scaled = (w * np.exp2(127.0 - byte)[:, None, :]).reshape(k, n).astype(np.float32)
    by_word = np.ascontiguousarray(scaled.reshape(k // 512, 128, 4, n).transpose(0, 1, 3, 2))
    if fmt == "e4m3":
        words = by_word.astype(ml_dtypes.float8_e4m3fn).view(np.uint8)
    else:
        c = by_word.astype(ml_dtypes.float4_e2m1fn).view(np.uint8) & 0xF
        words = (c[..., 0::2] | (c[..., 1::2] << 4)).reshape(k // 512, 128, 2 * n)
    return np.ascontiguousarray(words), np.ascontiguousarray(byte.astype(np.uint8).reshape(k // 512, 16, n))


def unpack_weight(words, scales, fmt):
    g, _, n = scales.shape
    words = np.ascontiguousarray(words).reshape(g, 128, n, -1)
    if fmt == "e4m3":
        vals = words.view(ml_dtypes.float8_e4m3fn).astype(np.float64)
    else:
        nib = np.empty((g, 128, n, 4), np.uint8)
        nib[..., 0::2] = words & 0xF
        nib[..., 1::2] = words >> 4
        vals = E2M1[nib]
    vals = vals * np.repeat(np.exp2(scales.astype(np.float64) - 127.0), 8, axis=1)[..., None]
    return vals.transpose(0, 1, 3, 2).reshape(g * 512, n)


def gelu(v):
    return 0.5 * v * (1.0 + np.tanh(np.sqrt(2.0 / np.pi) * (v + 0.044715 * v**3)))


K, T, S, P, H, G, N = 1024, 4096, 1024, 512, 512, 1024, 768

def setup_inputs():
    n = np.random.standard_normal
    s = mx_kscale(K)[:, None]
    u = mx_kscale(H)[:, None]
    tab_words, tab_scales = pack_weight(n((K, T)) * s, "e4m3")
    w1 = n((K, G)) / np.sqrt(K) / s
    w1[:, :H] *= u.T
    wc_words, wc_scales = pack_weight(2.0 * n((H, N)) / np.sqrt(H) / u, "e2m1")
    wv = n((H, N)) / np.sqrt(H) / u
    return {
        "tab_words": tab_words, "tab_scales": tab_scales,
        "offs": striped(np.random.permutation(T)[:S]),
        "w1": w1.astype(np.float32),
        "pos1": striped(np.random.permutation(S)[:P]),
        "pos2": striped(np.random.permutation(S)[:P]),
        "wc_words": wc_words, "wc_scales": wc_scales,
        "wv": wv.astype(np.float32),
    }

def reference(tab_words, tab_scales, offs, w1, pos1, pos2, wc_words, wc_scales, wv):
    v = unpack_weight(tab_words, tab_scales, "e4m3")[:, unstriped(offs)]
    w1q = mxq(f64(w1), 0, "e4m3")
    h = w1q.T @ v
    a = h[:H][:, unstriped(pos1)]
    b = h[H:][:, unstriped(pos2)]
    z = a * (1.0 / (1.0 + np.exp(-b)))
    zq = mxq(z, 0, "e4m3")
    wc = unpack_weight(wc_words, wc_scales, "e2m1")
    wvq = mxq(f64(wv), 0, "e4m3")
    click = 1.0 / (1.0 + np.exp(-(wc.T @ zq)))
    value = np.exp(wvq.T @ zq)
    return click * value

@@ -1,0 +1,285 @@
+from contextlib import ExitStack
+
+import concourse.mybir as mybir
+
+K, T, S, PAIRS, H, G, N = 1024, 4096, 1024, 512, 512, 1024, 768
+FLOPS = 2 * K * G * S + 4 * H * N * PAIRS
+
+F32 = mybir.dt.float32
+BF16 = mybir.dt.bfloat16
+I32 = mybir.dt.int32
+U32 = mybir.dt.uint32
+U16 = mybir.dt.uint16
+U8 = mybir.dt.uint8
+FP8X4 = mybir.dt.float8_e4m3fn_x4
+FP4X4 = mybir.dt.float4_e2m1fn_x4
+ACT = mybir.ActivationFunctionType
+ALU = mybir.AluOpType
+
+P = 128
+PACK = 4
+KP = 512
+BANK = 512
+LN_HALF = -0.6931471805599453
+CTX, AD = 1, 0
+CHUNKS = [256,256]
+
+
+def tile_list_ad_auction_bids_kernel(tc, tab_words, tab_scales, offs, w1, pos1, pos2, wc_words, wc_scales, wv, out):
+    nc = tc.nc
+    with ExitStack() as ctx:
+        keep = ctx.enter_context(tc.tile_pool(name="keep", bufs=1))
+        ring = ctx.enter_context(tc.tile_pool(name="ring", bufs=3))
+        psum = ctx.enter_context(tc.psum_pool(name="psum", bufs=8))
+
+        def held(name, shape, dtype):
+            return keep.tile(shape, dtype, name=name, align_bytes=64)
+
+        offs_sb = keep.tile([P, S // 16], U16, name="offs_sb")
+        pos1_sb = keep.tile([P, PAIRS // 16], U16, name="pos1_sb")
+        pos2_sb = keep.tile([P, PAIRS // 16], U16, name="pos2_sb")
+
+        tab_sc = held("tab_sc", [P, T // 4], I32)
+        wc_sc = held("wc_sc", [P, N // 4], I32)
+        nc.vector.memset(tab_sc[:], 0)
+        nc.vector.memset(wc_sc[:], 0)
+        warm = held("warm", [P, 16], F32)
+        nc.vector.memset(warm[:, 0:8], 0.0)
+        nc.scalar.activation(warm[:, 8:16], warm[:, 0:8], ACT.Sigmoid)
+
+        tab = [held("tab%d" % a, [P, T], I32) for a in range(2)]
+        raw = {}
+        for half in (CTX, AD):
+            for a in range(2):
+                raw[half, a] = held("raw%d%d" % (half, a), [P, PACK, H], F32)
+        wv_raw = held("wv_raw", [P, PACK, N], F32)
+        wc_codes = held("wc_codes", [P, 2 * N], U8)
+
+        def load_w1(half, a, c0, c1):
+            rows = w1[KP * a : KP * (a + 1), half * H + c0 : half * H + c1]
+            nc.sync.dma_start(out=raw[half, a][:, :, c0:c1], in_=rows.rearrange("(p j) c -> p j c", j=PACK))
+
+        def load_tab(a):
+            nc.sync.dma_start(out=tab[a][:], in_=tab_words[a].rearrange("p n t -> p (n t)").bitcast(I32))
+
+        ts32 = tab_scales.bitcast(I32)
+        ws32 = wc_scales.bitcast(I32)
+        for q in range(4):
+            nc.gpsimd.dma_start(out=tab_sc[32 * q : 32 * q + 8, :], in_=ts32[:, 4 * q : 4 * q + 4, :])
+        for q in range(4):
+            nc.gpsimd.dma_start(out=wc_sc[32 * q : 32 * q + 4, :], in_=ws32[0, 4 * q : 4 * q + 4, :])
+
+        nc.sync.dma_start(offs_sb[:], offs)
+        load_tab(0)
+        load_w1(CTX, 0, 0, H)
+        load_tab(1)
+        load_w1(CTX, 1, 0, 256)
+        load_w1(CTX, 1, 256, H)
+        load_w1(AD, 0, 0, H)
+        load_w1(AD, 1, 0, H)
+        nc.sync.dma_start(pos2_sb[:], pos2)
+        nc.sync.dma_start(pos1_sb[:], pos1)
+        nc.sync.dma_start(out=wv_raw[:], in_=wv.rearrange("(p j) c -> p j c", j=PACK))
+        nc.sync.dma_start(out=wc_codes[:].bitcast(I32), in_=wc_words[0].bitcast(I32))
+
+        grouped, w1_codes, w1_sc = {}, {}, {}
+        for half in (CTX, AD):
+            for a in range(2):
+                grouped[half, a] = held("grp%d%d" % (half, a), [P, PACK * H], BF16)
+                w1_codes[half, a] = held("w1c%d%d" % (half, a), [P, H], U32)
+                w1_sc[half, a] = held("w1s%d%d" % (half, a), [P, H], U8)
+
+        def cast(eng, dst, src):
+            if eng == "v":
+                nc.vector.tensor_copy(out=dst, in_=src)
+            elif eng == "s":
+                nc.scalar.copy(out=dst, in_=src)
+            else:
+                nc.gpsimd.tensor_scalar(dst, src, 1.0, 0.0, ALU.mult, ALU.add)
+
+        def cast_w1(eng, half, a, m0, m1):
+            dst = grouped[half, a][:].rearrange("p (t m j) -> p m t j", t=PACK, j=PACK)[:, m0:m1]
+            src = raw[half, a][:].rearrange("p j (m t) -> p m t j", t=PACK)[:, m0:m1]
+            cast(eng, dst, src)
+
+        def quant_w1(half, a, t0, t1):
+            nc.vector.quantize_mx(
+                out=w1_codes[half, a][:, P * t0 : P * t1].bitcast(FP8X4),
+                scales=w1_sc[half, a][:, P * t0 : P * t1],
+                in_=grouped[half, a][:, KP * t0 : KP * t1],
+            )
+
+        got = [held("got%d" % a, [P, S], U32) for a in range(2)]
+        got_sc = held("got_sc", [P, S], U8)
+
+        def gather_tab(a, i0, i1):
+            nc.vector.tensor_copy(got[a][:, i0:i1], tab[a][:].bitcast(U32).indirect(offs_sb[:, i0 // 16 : i1 // 16]))
+
+        def gather_sc():
+            nc.vector.tensor_copy(got_sc[:], tab_sc[:].bitcast(U8).indirect(offs_sb[:]))
+
+        acc = {}
+
+        def mm1(half, t, ih, a):
+            if a == 0:
+                acc[half, t, ih] = psum.tile([P, BANK], F32, name="bank")
+            cols = slice(BANK * ih, BANK * (ih + 1))
+            nc.tensor.matmul_mx(
+                out=acc[half, t, ih][:],
+                lhsT=w1_codes[half, a][:, P * t : P * (t + 1)].bitcast(FP8X4),
+                lhsT_scale=w1_sc[half, a][:, P * t : P * (t + 1)],
+                rhs=got[a][:, cols].bitcast(FP8X4),
+                rhs_scale=got_sc[4 * a : P, cols],
+                start=(a == 0),
+                stop=(a == 1),
+            )
+
+        h = {}
+        for half in (CTX, AD):
+            for t in range(PACK):
+                h[half, t] = held("h%d%d" % (half, t), [P, S], F32)
+
+        def h_out(eng, half, t, ih):
+            dst = h[half, t][:, BANK * ih : BANK * (ih + 1)]
+            if eng == "v":
+                nc.vector.tensor_copy(out=dst, in_=acc[half, t, ih][:])
+            else:
+                nc.scalar.copy(out=dst, in_=acc[half, t, ih][:])
+
+        picked = held("picked", [P, PACK, PAIRS], F32)
+        gate = held("gate", [P, PACK, PAIRS], F32)
+
+        def gather_ctx(t):
+            nc.vector.tensor_copy(picked[:, t, :], h[CTX, t][:].indirect(pos2_sb[:]))
+
+        def sigmoid_ctx(t):
+            nc.scalar.activation(gate[:, t, :], picked[:, t, :], ACT.Sigmoid)
+
+        wv_grp = held("wv_grp", [P, N, PACK], BF16)
+        wv_codes = held("wv_codes", [P, N], U32)
+        wv_sc = held("wv_sc", [P, N], U8)
+
+        def cast_wv(eng, c0, c1):
+            cast(eng, wv_grp[:, c0:c1, :], wv_raw[:, :, c0:c1].rearrange("p j c -> p c j"))
+
+        def quant_wv(c0, c1):
+            nc.vector.quantize_mx(
+                out=wv_codes[:, c0:c1].bitcast(FP8X4),
+                scales=wv_sc[:, c0:c1],
+                in_=wv_grp[:, c0:c1, :].rearrange("p c j -> p (c j)"),
+            )
+
+        starts = [sum(CHUNKS[:c]) for c in range(len(CHUNKS))]
+        z32 = [held("z32_%d" % c, [P, PACK, n], F32) for c, n in enumerate(CHUNKS)]
+        z16 = [held("z16_%d" % c, [P, n, PACK], BF16) for c, n in enumerate(CHUNKS)]
+        z_codes = [held("zc_%d" % c, [P, n], U32) for c, n in enumerate(CHUNKS)]
+        z_sc = [held("zs_%d" % c, [P, n], U8) for c, n in enumerate(CHUNKS)]
+
+        def gather_ad(c, t):
+            j0, n = starts[c], CHUNKS[c]
+            nc.vector.tensor_tensor(
+                z32[c][:, t, :], h[AD, t][:].indirect(pos1_sb[:, j0 // 16 : (j0 + n) // 16]), gate[:, t, j0 : j0 + n], ALU.mult
+            )
+
+        def cast_z(eng, c, n0, n1):
+            cast(eng, z16[c][:, n0:n1, :], z32[c][:, :, n0:n1].rearrange("p t n -> p n t"))
+
+        def quant_z(c):
+            nc.vector.quantize_mx(
+                out=z_codes[c][:].bitcast(FP8X4), scales=z_sc[c][:], in_=z16[c][:].rearrange("p n t -> p (n t)")
+            )
+
+        wc_sc8 = wc_sc[:].bitcast(U8)
+
+        def stage2(c, u):
+            j0, n = starts[c], CHUNKS[c]
+            per = BANK // n
+            value = psum.tile([P, per, n], F32, name="bank")
+            click = psum.tile([P, per, n], F32, name="bank")
+            for i in range(per):
+                cols = slice(P * (per * u + i), P * (per * u + i + 1))
+                nc.tensor.matmul_mx(
+                    out=value[:, i, :], lhsT=wv_codes[:, cols].bitcast(FP8X4), lhsT_scale=wv_sc[:, cols],
+                    rhs=z_codes[c][:].bitcast(FP8X4), rhs_scale=z_sc[c][:], start=True, stop=True,
+                )
+            for i in range(per):
+                cols = slice(P * (per * u + i), P * (per * u + i + 1))
+                nc.tensor.matmul_mx(
+                    out=click[:, i, :], lhsT=wc_codes[:, 2 * cols.start : 2 * cols.stop].bitcast(FP4X4), lhsT_scale=wc_sc8[:, cols],
+                    rhs=z_codes[c][:].bitcast(FP8X4), rhs_scale=z_sc[c][:], start=True, stop=True,
+                )
+            half_exp = ring.tile([P, per, n], F32, name="half_exp")
+            tanh = ring.tile([P, per, n], F32, name="tanh")
+            bid = ring.tile([P, per, n], F32, name="bid")
+            nc.scalar.activation(half_exp[:], value[:], ACT.Exp, bias=LN_HALF)
+            nc.scalar.activation(tanh[:], click[:], ACT.Tanh, scale=0.5)
+            nc.vector.scalar_tensor_tensor(bid[:], tanh[:], 1.0, half_exp[:], ALU.add, ALU.mult)
+            rows = out[P * per * u : P * per * (u + 1), j0 : j0 + n]
+            nc.sync.dma_start(out=rows.rearrange("(i p) c -> p i c", p=P), in_=bid[:])
+
+        gather_tab(0, 0, S)
+        cast_w1("s", CTX, 0, 0, P)
+        gather_sc()
+        quant_w1(CTX, 0, 0, 4)
+        for t in range(PACK):
+            for ih in range(2):
+                mm1(CTX, t, ih, 0)
+        gather_tab(1, 0, BANK)
+        gather_tab(1, BANK, S)
+        cast_w1("s", CTX, 1, 0, 64)
+        cast_w1("v", CTX, 1, 64, P)
+        for t in range(PACK):
+            quant_w1(CTX, 1, t, t + 1)
+        for t in range(PACK):
+            for ih in range(2):
+                mm1(CTX, t, ih, 1)
+        h_out("v", CTX, 0, 1)
+        for t in range(PACK):
+            for ih in range(2):
+                if (t, ih) != (0, 1):
+                    h_out("s", CTX, t, ih)
+        gather_ctx(0)
+        cast_w1("v", AD, 0, 0, P)
+        gather_ctx(1)
+        quant_w1(AD, 0, 0, 4)
+        for t in range(PACK):
+            for ih in range(2):
+                mm1(AD, t, ih, 0)
+        cast_w1("s", AD, 1, 0, 64)
+        cast_w1("v", AD, 1, 64, P)
+        gather_ctx(2)
+        quant_w1(AD, 1, 0, 2)
+        quant_w1(AD, 1, 2, 4)
+        gather_ctx(3)
+        for t in range(PACK):
+            sigmoid_ctx(t)
+        for t in range(PACK):
+            for ih in range(2):
+                mm1(AD, t, ih, 1)
+        h_out("v", AD, 0, 1)
+        for t in range(PACK):
+            for ih in range(2):
+                if (t, ih) != (0, 1):
+                    h_out("s", AD, t, ih)
+        cast_wv("v", 0, 256)
+        gather_ad(0, 0)
+        quant_wv(0, 256)
+        cast_wv("s", 256, 512)
+        cast_wv("s", 512, 768)
+        for t in range(1, PACK):
+            gather_ad(0, t)
+        cast_z("v", 0, 0, 256)
+        gather_ad(1, 0)
+        quant_z(0)
+        quant_wv(256, 512)
+        gather_ad(1, 1)
+        quant_wv(512, 768)
+        for t in range(2, PACK):
+            gather_ad(1, t)
+        cast_z("v", 1, 0, 256)
+        stage2(0, 0)
+        quant_z(1)
+        stage2(0, 1)
+        stage2(0, 2)
+        for u in range(3):
+            stage2(1, u)

@@ -29,7 +29,6 @@ def tile_list_ad_auction_bids_kernel(tc, tab_words, tab_scales, offs, w1, pos1, 
     nc = tc.nc
     with ExitStack() as ctx:
         keep = ctx.enter_context(tc.tile_pool(name="keep", bufs=1))
-        ring = ctx.enter_context(tc.tile_pool(name="ring", bufs=3))
         psum = ctx.enter_context(tc.psum_pool(name="psum", bufs=8))
 
         def held(name, shape, dtype):
@@ -64,23 +63,43 @@ def tile_list_ad_auction_bids_kernel(tc, tab_words, tab_scales, offs, w1, pos1, 
 
         ts32 = tab_scales.bitcast(I32)
         ws32 = wc_scales.bitcast(I32)
-        for q in range(4):
-            nc.gpsimd.dma_start(out=tab_sc[32 * q : 32 * q + 8, :], in_=ts32[:, 4 * q : 4 * q + 4, :])
-        for q in range(4):
-            nc.gpsimd.dma_start(out=wc_sc[32 * q : 32 * q + 4, :], in_=ws32[0, 4 * q : 4 * q + 4, :])
 
-        nc.sync.dma_start(offs_sb[:], offs)
-        load_tab(0)
+        def load_tab_sc(a, r):
+            nc.sync.dma_start(out=tab_sc[4 * a + r : P : 32, :], in_=ts32[a, r:16:4, :])
+
+        def load_wc_sc(q):
+            nc.sync.dma_start(out=wc_sc[32 * q : 32 * q + 4, :], in_=ws32[0, 4 * q : 4 * q + 4, :])
+
+        lists = {"offs": (offs_sb, offs), "pos1": (pos1_sb, pos1), "pos2": (pos2_sb, pos2)}
+
+        def load_list(name):
+            nc.sync.dma_start(lists[name][0][:], lists[name][1])
+
+        def load_wv(c0=0, c1=N):
+            nc.sync.dma_start(out=wv_raw[:, :, c0:c1], in_=wv[:, c0:c1].rearrange("(p j) c -> p j c", j=PACK))
+
+        def load_wc():
+            nc.sync.dma_start(out=wc_codes[:].bitcast(I32), in_=wc_words[0].bitcast(I32))
+
         load_w1(CTX, 0, 0, H)
+        load_list("offs")
+        for r in range(4):
+            load_tab_sc(0, r)
+        load_tab(0)
+        for r in range(4):
+            load_tab_sc(1, r)
         load_tab(1)
+        load_list("pos2")
         load_w1(CTX, 1, 0, 256)
         load_w1(CTX, 1, 256, H)
         load_w1(AD, 0, 0, H)
-        load_w1(AD, 1, 0, H)
-        nc.sync.dma_start(pos2_sb[:], pos2)
-        nc.sync.dma_start(pos1_sb[:], pos1)
-        nc.sync.dma_start(out=wv_raw[:], in_=wv.rearrange("(p j) c -> p j c", j=PACK))
-        nc.sync.dma_start(out=wc_codes[:].bitcast(I32), in_=wc_words[0].bitcast(I32))
+        load_w1(AD, 1, 0, 256)
+        load_w1(AD, 1, 256, H)
+        load_list("pos1")
+        load_wv()
+        load_wc()
+        for q in range(4):
+            load_wc_sc(q)
 
         grouped, w1_codes, w1_sc = {}, {}, {}
         for half in (CTX, AD):
@@ -191,41 +210,42 @@ def tile_list_ad_auction_bids_kernel(tc, tab_words, tab_scales, offs, w1, pos1, 
 
         wc_sc8 = wc_sc[:].bitcast(U8)
 
-        def stage2(c, u):
+        acts = {}
+
+        def s2mm(kind, c, n0, n1):
+            n = CHUNKS[c]
+            bank = psum.tile([P, n1 - n0, n], F32, name="bank")
+            for m in range(n0, n1):
+                cols = slice(P * m, P * (m + 1))
+                if kind == "val":
+                    codes, scales = wv_codes[:, cols].bitcast(FP8X4), wv_sc[:, cols]
+                else:
+                    codes, scales = wc_codes[:, 2 * cols.start : 2 * cols.stop].bitcast(FP4X4), wc_sc8[:, cols]
+                nc.tensor.matmul_mx(
+                    out=bank[:, m - n0, :], lhsT=codes, lhsT_scale=scales,
+                    rhs=z_codes[c][:].bitcast(FP8X4), rhs_scale=z_sc[c][:], start=True, stop=True,
+                )
+            acts[kind, c, n0] = held("act_%s%d%d" % (kind, c, n0), [P, n1 - n0, n], F32)
+            if kind == "val":
+                nc.scalar.activation(acts[kind, c, n0][:], bank[:], ACT.Exp, bias=LN_HALF)
+            else:
+                nc.scalar.activation(acts[kind, c, n0][:], bank[:], ACT.Tanh, scale=0.5)
+
+        def s2mul(c, n0, n1):
             j0, n = starts[c], CHUNKS[c]
-            per = BANK // n
-            value = psum.tile([P, per, n], F32, name="bank")
-            click = psum.tile([P, per, n], F32, name="bank")
-            for i in range(per):
-                cols = slice(P * (per * u + i), P * (per * u + i + 1))
-                nc.tensor.matmul_mx(
-                    out=value[:, i, :], lhsT=wv_codes[:, cols].bitcast(FP8X4), lhsT_scale=wv_sc[:, cols],
-                    rhs=z_codes[c][:].bitcast(FP8X4), rhs_scale=z_sc[c][:], start=True, stop=True,
-                )
-            for i in range(per):
-                cols = slice(P * (per * u + i), P * (per * u + i + 1))
-                nc.tensor.matmul_mx(
-                    out=click[:, i, :], lhsT=wc_codes[:, 2 * cols.start : 2 * cols.stop].bitcast(FP4X4), lhsT_scale=wc_sc8[:, cols],
-                    rhs=z_codes[c][:].bitcast(FP8X4), rhs_scale=z_sc[c][:], start=True, stop=True,
-                )
-            half_exp = ring.tile([P, per, n], F32, name="half_exp")
-            tanh = ring.tile([P, per, n], F32, name="tanh")
-            bid = ring.tile([P, per, n], F32, name="bid")
-            nc.scalar.activation(half_exp[:], value[:], ACT.Exp, bias=LN_HALF)
-            nc.scalar.activation(tanh[:], click[:], ACT.Tanh, scale=0.5)
-            nc.vector.scalar_tensor_tensor(bid[:], tanh[:], 1.0, half_exp[:], ALU.add, ALU.mult)
-            rows = out[P * per * u : P * per * (u + 1), j0 : j0 + n]
+            bid = held("bid%d%d" % (c, n0), [P, n1 - n0, n], F32)
+            nc.vector.scalar_tensor_tensor(bid[:], acts["clk", c, n0][:], 1.0, acts["val", c, n0][:], ALU.add, ALU.mult)
+            rows = out[P * n0 : P * n1, j0 : j0 + n]
             nc.sync.dma_start(out=rows.rearrange("(i p) c -> p i c", p=P), in_=bid[:])
 
-        gather_tab(0, 0, S)
         cast_w1("s", CTX, 0, 0, P)
-        gather_sc()
         quant_w1(CTX, 0, 0, 4)
+        gather_tab(0, 0, S)
+        gather_sc()
         for t in range(PACK):
             for ih in range(2):
                 mm1(CTX, t, ih, 0)
-        gather_tab(1, 0, BANK)
-        gather_tab(1, BANK, S)
+        gather_tab(1, 0, S)
         cast_w1("s", CTX, 1, 0, 64)
         cast_w1("v", CTX, 1, 64, P)
         for t in range(PACK):
@@ -233,53 +253,51 @@ def tile_list_ad_auction_bids_kernel(tc, tab_words, tab_scales, offs, w1, pos1, 
         for t in range(PACK):
             for ih in range(2):
                 mm1(CTX, t, ih, 1)
-        h_out("v", CTX, 0, 1)
         for t in range(PACK):
-            for ih in range(2):
-                if (t, ih) != (0, 1):
-                    h_out("s", CTX, t, ih)
+            h_out("s", CTX, t, 0)
+            h_out("v" if t < 0 else "s", CTX, t, 1)
+        cast_w1("v", AD, 0, 0, 64)
+        cast_w1("v", AD, 0, 64, P)
         gather_ctx(0)
-        cast_w1("v", AD, 0, 0, P)
-        gather_ctx(1)
         quant_w1(AD, 0, 0, 4)
+        cast_w1("s", AD, 1, 0, 64)
+        cast_w1("v", AD, 1, 64, P)
+        gather_ctx(1)
+        quant_w1(AD, 1, 0, 2)
+        quant_w1(AD, 1, 2, 4)
         for t in range(PACK):
             for ih in range(2):
                 mm1(AD, t, ih, 0)
-        cast_w1("s", AD, 1, 0, 64)
-        cast_w1("v", AD, 1, 64, P)
+                mm1(AD, t, ih, 1)
         gather_ctx(2)
-        quant_w1(AD, 1, 0, 2)
-        quant_w1(AD, 1, 2, 4)
         gather_ctx(3)
         for t in range(PACK):
             sigmoid_ctx(t)
+            h_out("s", AD, t, 0)
+            h_out("v" if t >= 4 - 1 else "s", AD, t, 1)
+        cast_wv("s", 0, 256)
         for t in range(PACK):
-            for ih in range(2):
-                mm1(AD, t, ih, 1)
-        h_out("v", AD, 0, 1)
-        for t in range(PACK):
-            for ih in range(2):
-                if (t, ih) != (0, 1):
-                    h_out("s", AD, t, ih)
-        cast_wv("v", 0, 256)
-        gather_ad(0, 0)
-        quant_wv(0, 256)
-        cast_wv("s", 256, 512)
-        cast_wv("s", 512, 768)
-        for t in range(1, PACK):
             gather_ad(0, t)
-        cast_z("v", 0, 0, 256)
-        gather_ad(1, 0)
+        cast_z("s", 0, 0, 128)
+        cast_z("v", 0, 128, 256)
+        quant_wv(0, 256)
         quant_z(0)
+        cast_wv("v", 256, 512)
+        cast_wv("v", 512, 768)
+        gather_ad(1, 0)
         quant_wv(256, 512)
         gather_ad(1, 1)
         quant_wv(512, 768)
         for t in range(2, PACK):
             gather_ad(1, t)
         cast_z("v", 1, 0, 256)
-        stage2(0, 0)
-        quant_z(1)
-        stage2(0, 1)
-        stage2(0, 2)
         for u in range(3):
-            stage2(1, u)
+            s2mm("val", 0, 2*u, 2*u+2)
+            s2mm("clk", 0, 2*u, 2*u+2)
+        quant_z(1)
+        for u in range(3):
+            s2mul(0, 2*u, 2*u+2)
+        for u in range(3):
+            s2mm("val", 1, 2*u, 2*u+2)
+            s2mm("clk", 1, 2*u, 2*u+2)
+            s2mul(1, 2*u, 2*u+2)

@@ -47,16 +47,16 @@ def tile_list_ad_auction_bids_kernel(tc, tab_words, tab_scales, offs, w1, pos1, 
         nc.scalar.activation(warm[:, 8:16], warm[:, 0:8], ACT.Sigmoid)
 
         tab = [held("tab%d" % a, [P, T], I32) for a in range(2)]
-        raw = {}
-        for half in (CTX, AD):
-            for a in range(2):
-                raw[half, a] = held("raw%d%d" % (half, a), [P, PACK, H], F32)
+        raw = [held("raw%d" % a, [P, PACK, G], F32) for a in range(2)]
         wv_raw = held("wv_raw", [P, PACK, N], F32)
         wc_codes = held("wc_codes", [P, 2 * N], U8)
 
         def load_w1(half, a, c0, c1):
             rows = w1[KP * a : KP * (a + 1), half * H + c0 : half * H + c1]
-            nc.sync.dma_start(out=raw[half, a][:, :, c0:c1], in_=rows.rearrange("(p j) c -> p j c", j=PACK))
+            nc.sync.dma_start(out=raw[a][:, :, half * H + c0 : half * H + c1], in_=rows.rearrange("(p j) c -> p j c", j=PACK))
+
+        def load_w1p(a):
+            nc.sync.dma_start(out=raw[a][:], in_=w1[KP * a : KP * (a + 1), :].rearrange("(p j) c -> p j c", j=PACK))
 
         def load_tab(a):
             nc.sync.dma_start(out=tab[a][:], in_=tab_words[a].rearrange("p n t -> p (n t)").bitcast(I32))
@@ -81,20 +81,21 @@ def tile_list_ad_auction_bids_kernel(tc, tab_words, tab_scales, offs, w1, pos1, 
         def load_wc():
             nc.sync.dma_start(out=wc_codes[:].bitcast(I32), in_=wc_words[0].bitcast(I32))
 
-        load_w1(CTX, 0, 0, H)
+        load_w1p(0)
         load_list("offs")
-        for r in range(4):
-            load_tab_sc(0, r)
+        load_tab_sc(0, 0)
+        load_tab_sc(1, 0)
+        load_tab_sc(0, 1)
+        load_tab_sc(1, 1)
         load_tab(0)
-        for r in range(4):
-            load_tab_sc(1, r)
-        load_tab(1)
+        load_tab_sc(0, 2)
+        load_tab_sc(1, 2)
+        load_tab_sc(0, 3)
+        load_tab_sc(1, 3)
+        load_w1(CTX,1,0,H)
         load_list("pos2")
-        load_w1(CTX, 1, 0, 256)
-        load_w1(CTX, 1, 256, H)
-        load_w1(AD, 0, 0, H)
-        load_w1(AD, 1, 0, 256)
-        load_w1(AD, 1, 256, H)
+        load_tab(1)
+        load_w1(AD,1,0,H)
         load_list("pos1")
         load_wv()
         load_wc()
@@ -118,7 +119,7 @@ def tile_list_ad_auction_bids_kernel(tc, tab_words, tab_scales, offs, w1, pos1, 
 
         def cast_w1(eng, half, a, m0, m1):
             dst = grouped[half, a][:].rearrange("p (t m j) -> p m t j", t=PACK, j=PACK)[:, m0:m1]
-            src = raw[half, a][:].rearrange("p j (m t) -> p m t j", t=PACK)[:, m0:m1]
+            src = raw[a][:, :, half * H : (half + 1) * H].rearrange("p j (m t) -> p m t j", t=PACK)[:, m0:m1]
             cast(eng, dst, src)
 
         def quant_w1(half, a, t0, t1):
@@ -179,7 +180,7 @@ def tile_list_ad_auction_bids_kernel(tc, tab_words, tab_scales, offs, w1, pos1, 
         wv_sc = held("wv_sc", [P, N], U8)
 
         def cast_wv(eng, c0, c1):
-            cast(eng, wv_grp[:, c0:c1, :], wv_raw[:, :, c0:c1].rearrange("p j c -> p c j"))
+            cast(eng, wv_grp[:, c0:c1, :].rearrange("p (c i) j -> p c j i", i=4), wv_raw[:, :, c0:c1].rearrange("p j (c i) -> p c j i", i=4))
 
         def quant_wv(c0, c1):
             nc.vector.quantize_mx(
@@ -201,7 +202,7 @@ def tile_list_ad_auction_bids_kernel(tc, tab_words, tab_scales, offs, w1, pos1, 
             )
 
         def cast_z(eng, c, n0, n1):
-            cast(eng, z16[c][:, n0:n1, :], z32[c][:, :, n0:n1].rearrange("p t n -> p n t"))
+            cast(eng, z16[c][:, n0:n1, :].rearrange("p (c i) j -> p c j i", i=4), z32[c][:, :, n0:n1].rearrange("p j (c i) -> p c j i", i=4))
 
         def quant_z(c):
             nc.vector.quantize_mx(
@@ -239,38 +240,34 @@ def tile_list_ad_auction_bids_kernel(tc, tab_words, tab_scales, offs, w1, pos1, 
             nc.sync.dma_start(out=rows.rearrange("(i p) c -> p i c", p=P), in_=bid[:])
 
         cast_w1("s", CTX, 0, 0, P)
+        cast_w1("v", AD, 0, 0, P)
+        quant_w1(AD, 0, 0, 4)
         quant_w1(CTX, 0, 0, 4)
         gather_tab(0, 0, S)
         gather_sc()
-        for t in range(PACK):
-            for ih in range(2):
+        cast_w1("s", CTX, 1, 0, P)
+        quant_w1(CTX, 1, 0, 4)
+        for ih in range(2):
+            for t in range(PACK):
                 mm1(CTX, t, ih, 0)
-        gather_tab(1, 0, S)
-        cast_w1("s", CTX, 1, 0, 64)
-        cast_w1("v", CTX, 1, 64, P)
-        for t in range(PACK):
-            quant_w1(CTX, 1, t, t + 1)
-        for t in range(PACK):
-            for ih in range(2):
+        for ih in range(2):
+            gather_tab(1, BANK*ih, BANK*ih+BANK)
+            for t in range(PACK):
                 mm1(CTX, t, ih, 1)
+        cast_w1("v", AD, 1, 0, 64)
+        cast_w1("v", AD, 1, 64, P)
         for t in range(PACK):
             h_out("s", CTX, t, 0)
-            h_out("v" if t < 0 else "s", CTX, t, 1)
-        cast_w1("v", AD, 0, 0, 64)
-        cast_w1("v", AD, 0, 64, P)
-        gather_ctx(0)
-        quant_w1(AD, 0, 0, 4)
-        cast_w1("s", AD, 1, 0, 64)
-        cast_w1("v", AD, 1, 64, P)
-        gather_ctx(1)
         quant_w1(AD, 1, 0, 2)
         quant_w1(AD, 1, 2, 4)
+        for t in range(PACK):
+            h_out("v" if t < 1 else "s", CTX, t, 1)
         for t in range(PACK):
             for ih in range(2):
                 mm1(AD, t, ih, 0)
                 mm1(AD, t, ih, 1)
-        gather_ctx(2)
-        gather_ctx(3)
+        for t in range(PACK):
+            gather_ctx(t)
         for t in range(PACK):
             sigmoid_ctx(t)
             h_out("s", AD, t, 0)
@@ -278,11 +275,11 @@ def tile_list_ad_auction_bids_kernel(tc, tab_words, tab_scales, offs, w1, pos1, 
         cast_wv("s", 0, 256)
         for t in range(PACK):
             gather_ad(0, t)
-        cast_z("s", 0, 0, 128)
+        cast_z("v", 0, 0, 128)
         cast_z("v", 0, 128, 256)
         quant_wv(0, 256)
         quant_z(0)
-        cast_wv("v", 256, 512)
+        cast_wv("s", 256, 512)
         cast_wv("v", 512, 768)
         gather_ad(1, 0)
         quant_wv(256, 512)
@@ -297,7 +294,7 @@ def tile_list_ad_auction_bids_kernel(tc, tab_words, tab_scales, offs, w1, pos1, 
         quant_z(1)
         for u in range(3):
             s2mul(0, 2*u, 2*u+2)
-        for u in range(3):
-            s2mm("val", 1, 2*u, 2*u+2)
-            s2mm("clk", 1, 2*u, 2*u+2)
-            s2mul(1, 2*u, 2*u+2)
+        for n0, n1 in ((0, 2), (2, 4), (4, 5), (5, 6)):
+            s2mm("val", 1, n0, n1)
+            s2mm("clk", 1, n0, n1)
+            s2mul(1, n0, n1)

@@ -47,16 +47,16 @@ def tile_list_ad_auction_bids_kernel(tc, tab_words, tab_scales, offs, w1, pos1, 
         nc.scalar.activation(warm[:, 8:16], warm[:, 0:8], ACT.Sigmoid)
 
         tab = [held("tab%d" % a, [P, T], I32) for a in range(2)]
-        raw = [held("raw%d" % a, [P, PACK, G], F32) for a in range(2)]
+        raw = {}
+        for half in (CTX, AD):
+            for a in range(2):
+                raw[half, a] = held("raw%d%d" % (half, a), [P, PACK, H], F32)
         wv_raw = held("wv_raw", [P, PACK, N], F32)
         wc_codes = held("wc_codes", [P, 2 * N], U8)
 
         def load_w1(half, a, c0, c1):
             rows = w1[KP * a : KP * (a + 1), half * H + c0 : half * H + c1]
-            nc.sync.dma_start(out=raw[a][:, :, half * H + c0 : half * H + c1], in_=rows.rearrange("(p j) c -> p j c", j=PACK))
-
-        def load_w1p(a):
-            nc.sync.dma_start(out=raw[a][:], in_=w1[KP * a : KP * (a + 1), :].rearrange("(p j) c -> p j c", j=PACK))
+            nc.sync.dma_start(out=raw[half, a][:, :, c0:c1], in_=rows.rearrange("(p j) c -> p j c", j=PACK))
 
         def load_tab(a):
             nc.sync.dma_start(out=tab[a][:], in_=tab_words[a].rearrange("p n t -> p (n t)").bitcast(I32))
@@ -81,7 +81,7 @@ def tile_list_ad_auction_bids_kernel(tc, tab_words, tab_scales, offs, w1, pos1, 
         def load_wc():
             nc.sync.dma_start(out=wc_codes[:].bitcast(I32), in_=wc_words[0].bitcast(I32))
 
-        load_w1p(0)
+        load_w1(CTX,0,0,H)
         load_list("offs")
         load_tab_sc(0, 0)
         load_tab_sc(1, 0)
@@ -92,10 +92,11 @@ def tile_list_ad_auction_bids_kernel(tc, tab_words, tab_scales, offs, w1, pos1, 
         load_tab_sc(1, 2)
         load_tab_sc(0, 3)
         load_tab_sc(1, 3)
-        load_w1(CTX,1,0,H)
-        load_list("pos2")
         load_tab(1)
+        load_w1(CTX,1,0,H)
+        load_w1(AD,0,0,H)
         load_w1(AD,1,0,H)
+        load_list("pos2")
         load_list("pos1")
         load_wv()
         load_wc()
@@ -117,12 +118,12 @@ def tile_list_ad_auction_bids_kernel(tc, tab_words, tab_scales, offs, w1, pos1, 
             else:
                 nc.gpsimd.tensor_scalar(dst, src, 1.0, 0.0, ALU.mult, ALU.add)
 
-        def cast_w1(eng, half, a, m0, m1):
-            dst = grouped[half, a][:].rearrange("p (t m j) -> p m t j", t=PACK, j=PACK)[:, m0:m1]
-            src = raw[a][:, :, half * H : (half + 1) * H].rearrange("p j (m t) -> p m t j", t=PACK)[:, m0:m1]
+        def cast_w1t(eng, half, a, t0, t1):
+            dst = grouped[half, a][:, KP * t0 : KP * t1].rearrange("p (t m j) -> p m t j", m=P, j=PACK)
+            src = raw[half, a][:].rearrange("p j (m t) -> p m t j", t=PACK)[:, :, t0:t1, :]
             cast(eng, dst, src)
 
-        def quant_w1(half, a, t0, t1):
+        def quant_w1t(half, a, t0, t1):
             nc.vector.quantize_mx(
                 out=w1_codes[half, a][:, P * t0 : P * t1].bitcast(FP8X4),
                 scales=w1_sc[half, a][:, P * t0 : P * t1],
@@ -190,7 +191,7 @@ def tile_list_ad_auction_bids_kernel(tc, tab_words, tab_scales, offs, w1, pos1, 
             )
 
         starts = [sum(CHUNKS[:c]) for c in range(len(CHUNKS))]
-        z32 = [held("z32_%d" % c, [P, PACK, n], F32) for c, n in enumerate(CHUNKS)]
+        z32 = [held("z32", [P, PACK, CHUNKS[0]], F32)] * len(CHUNKS)
         z16 = [held("z16_%d" % c, [P, n, PACK], BF16) for c, n in enumerate(CHUNKS)]
         z_codes = [held("zc_%d" % c, [P, n], U32) for c, n in enumerate(CHUNKS)]
         z_sc = [held("zs_%d" % c, [P, n], U8) for c, n in enumerate(CHUNKS)]
@@ -239,47 +240,49 @@ def tile_list_ad_auction_bids_kernel(tc, tab_words, tab_scales, offs, w1, pos1, 
             rows = out[P * n0 : P * n1, j0 : j0 + n]
             nc.sync.dma_start(out=rows.rearrange("(i p) c -> p i c", p=P), in_=bid[:])
 
-        cast_w1("s", CTX, 0, 0, P)
-        cast_w1("v", AD, 0, 0, P)
-        quant_w1(AD, 0, 0, 4)
-        quant_w1(CTX, 0, 0, 4)
+        cast_w1t("s", CTX, 0, 0, 4)
+
+        quant_w1t(CTX, 0, 0, 4)
         gather_tab(0, 0, S)
         gather_sc()
-        cast_w1("s", CTX, 1, 0, P)
-        quant_w1(CTX, 1, 0, 4)
-        for ih in range(2):
-            for t in range(PACK):
+        for t in range(PACK):
+            for ih in range(2):
                 mm1(CTX, t, ih, 0)
-        for ih in range(2):
-            gather_tab(1, BANK*ih, BANK*ih+BANK)
-            for t in range(PACK):
+        gather_tab(1, 0, S)
+        cast_w1t("v", CTX, 1, 0, 2)
+        cast_w1t("s", CTX, 1, 2, 4)
+        quant_w1t(CTX, 1, 0, 2)
+        quant_w1t(CTX, 1, 2, 4)
+        for t in range(PACK):
+            for ih in range(2):
                 mm1(CTX, t, ih, 1)
-        cast_w1("v", AD, 1, 0, 64)
-        cast_w1("v", AD, 1, 64, P)
         for t in range(PACK):
             h_out("s", CTX, t, 0)
-        quant_w1(AD, 1, 0, 2)
-        quant_w1(AD, 1, 2, 4)
-        for t in range(PACK):
-            h_out("v" if t < 1 else "s", CTX, t, 1)
+            h_out("v" if t < 0 else "s", CTX, t, 1)
+        cast_w1t("v", AD, 0, 0, 4)
+
+        quant_w1t(AD, 0, 0, 4)
+        cast_w1t("v", AD, 1, 0, 4)
+
+        quant_w1t(AD, 1, 0, 2)
+        quant_w1t(AD, 1, 2, 4)
         for t in range(PACK):
             for ih in range(2):
                 mm1(AD, t, ih, 0)
                 mm1(AD, t, ih, 1)
         for t in range(PACK):
             gather_ctx(t)
-        for t in range(PACK):
             sigmoid_ctx(t)
             h_out("s", AD, t, 0)
-            h_out("v" if t >= 4 - 1 else "s", AD, t, 1)
+            h_out("v" if t >= 4 - 0 else "s", AD, t, 1)
         cast_wv("s", 0, 256)
         for t in range(PACK):
             gather_ad(0, t)
         cast_z("v", 0, 0, 128)
-        cast_z("v", 0, 128, 256)
+        cast_z("s", 0, 128, 256)
         quant_wv(0, 256)
         quant_z(0)
-        cast_wv("s", 256, 512)
+        cast_wv("v", 256, 512)
         cast_wv("v", 512, 768)
         gather_ad(1, 0)
         quant_wv(256, 512)

@@ -22,7 +22,8 @@ KP = 512
 BANK = 512
 LN_HALF = -0.6931471805599453
 CTX, AD = 1, 0
-CHUNKS = [256,256]
+CHUNKS = [256, 128, 128]
+WV_COLS = 256
 
 
 def tile_list_ad_auction_bids_kernel(tc, tab_words, tab_scales, offs, w1, pos1, pos2, wc_words, wc_scales, wv, out):
@@ -81,21 +82,19 @@ def tile_list_ad_auction_bids_kernel(tc, tab_words, tab_scales, offs, w1, pos1, 
         def load_wc():
             nc.sync.dma_start(out=wc_codes[:].bitcast(I32), in_=wc_words[0].bitcast(I32))
 
-        load_w1(CTX,0,0,H)
+        load_w1(CTX, 0, 0, H)
         load_list("offs")
-        load_tab_sc(0, 0)
-        load_tab_sc(1, 0)
-        load_tab_sc(0, 1)
-        load_tab_sc(1, 1)
+        for r in range(2):
+            for a in range(2):
+                load_tab_sc(a, r)
         load_tab(0)
-        load_tab_sc(0, 2)
-        load_tab_sc(1, 2)
-        load_tab_sc(0, 3)
-        load_tab_sc(1, 3)
+        for r in range(2, 4):
+            for a in range(2):
+                load_tab_sc(a, r)
         load_tab(1)
-        load_w1(CTX,1,0,H)
-        load_w1(AD,0,0,H)
-        load_w1(AD,1,0,H)
+        load_w1(CTX, 1, 0, H)
+        load_w1(AD, 0, 0, H)
+        load_w1(AD, 1, 0, H)
         load_list("pos2")
         load_list("pos1")
         load_wv()
@@ -104,9 +103,13 @@ def tile_list_ad_auction_bids_kernel(tc, tab_words, tab_scales, offs, w1, pos1, 
             load_wc_sc(q)
 
         grouped, w1_codes, w1_sc = {}, {}, {}
+        picked_tile = held("picked", [P, PACK * PAIRS], F32)
+        picked = picked_tile[:].rearrange("p (t j) -> p t j", t=PACK)
+        late = picked_tile[:].bitcast(BF16).rearrange("p (t x) -> p t x", t=PACK)[:, :, 0:KP]
         for half in (CTX, AD):
             for a in range(2):
-                grouped[half, a] = held("grp%d%d" % (half, a), [P, PACK * H], BF16)
+                if (half, a) != (AD, 1):
+                    grouped[half, a] = held("grp%d%d" % (half, a), [P, PACK * H], BF16)[:]
                 w1_codes[half, a] = held("w1c%d%d" % (half, a), [P, H], U32)
                 w1_sc[half, a] = held("w1s%d%d" % (half, a), [P, H], U8)
 
@@ -119,15 +122,18 @@ def tile_list_ad_auction_bids_kernel(tc, tab_words, tab_scales, offs, w1, pos1, 
                 nc.gpsimd.tensor_scalar(dst, src, 1.0, 0.0, ALU.mult, ALU.add)
 
         def cast_w1t(eng, half, a, t0, t1):
-            dst = grouped[half, a][:, KP * t0 : KP * t1].rearrange("p (t m j) -> p m t j", m=P, j=PACK)
-            src = raw[half, a][:].rearrange("p j (m t) -> p m t j", t=PACK)[:, :, t0:t1, :]
+            if (half, a) == (AD, 1):
+                dst = late[:, t0:t1, :].rearrange("p t (m j) -> p m j t", j=PACK)
+            else:
+                dst = grouped[half, a][:, KP * t0 : KP * t1].rearrange("p (t m j) -> p m j t", m=P, j=PACK)
+            src = raw[half, a][:].rearrange("p j (m t) -> p m j t", t=PACK)[:, :, :, t0:t1]
             cast(eng, dst, src)
 
         def quant_w1t(half, a, t0, t1):
             nc.vector.quantize_mx(
                 out=w1_codes[half, a][:, P * t0 : P * t1].bitcast(FP8X4),
                 scales=w1_sc[half, a][:, P * t0 : P * t1],
-                in_=grouped[half, a][:, KP * t0 : KP * t1],
+                in_=late[:, t0, :] if (half, a) == (AD, 1) else grouped[half, a][:, KP * t0 : KP * t1],
             )
 
         got = [held("got%d" % a, [P, S], U32) for a in range(2)]
@@ -167,31 +173,35 @@ def tile_list_ad_auction_bids_kernel(tc, tab_words, tab_scales, offs, w1, pos1, 
             else:
                 nc.scalar.copy(out=dst, in_=acc[half, t, ih][:])
 
-        picked = held("picked", [P, PACK, PAIRS], F32)
         gate = held("gate", [P, PACK, PAIRS], F32)
 
-        def gather_ctx(t):
+        def gather_ctx(picked, t):
             nc.vector.tensor_copy(picked[:, t, :], h[CTX, t][:].indirect(pos2_sb[:]))
 
         def sigmoid_ctx(t):
             nc.scalar.activation(gate[:, t, :], picked[:, t, :], ACT.Sigmoid)
 
-        wv_grp = held("wv_grp", [P, N, PACK], BF16)
+        wv_grp = [held("wv_grp%d" % u, [P, WV_COLS, PACK], BF16) for u in range(N // WV_COLS)]
         wv_codes = held("wv_codes", [P, N], U32)
         wv_sc = held("wv_sc", [P, N], U8)
 
-        def cast_wv(eng, c0, c1):
-            cast(eng, wv_grp[:, c0:c1, :].rearrange("p (c i) j -> p c j i", i=4), wv_raw[:, :, c0:c1].rearrange("p j (c i) -> p c j i", i=4))
+        def cast_wv(eng, u):
+            src = wv_raw[:, :, WV_COLS * u : WV_COLS * (u + 1)]
+            if eng == "g":
+                cast(eng, wv_grp[u][:], src.rearrange("p j c -> p c j"))
+            else:
+                cast(eng, wv_grp[u][:].rearrange("p (c i) j -> p c j i", i=4), src.rearrange("p j (c i) -> p c j i", i=4))
 
-        def quant_wv(c0, c1):
+        def quant_wv(u):
+            c0, c1 = WV_COLS * u, WV_COLS * (u + 1)
             nc.vector.quantize_mx(
                 out=wv_codes[:, c0:c1].bitcast(FP8X4),
                 scales=wv_sc[:, c0:c1],
-                in_=wv_grp[:, c0:c1, :].rearrange("p c j -> p (c j)"),
+                in_=wv_grp[u][:].rearrange("p c j -> p (c j)"),
             )
 
         starts = [sum(CHUNKS[:c]) for c in range(len(CHUNKS))]
-        z32 = [held("z32", [P, PACK, CHUNKS[0]], F32)] * len(CHUNKS)
+        z32 = [held("z32", [P, PACK, max(CHUNKS)], F32)] * len(CHUNKS)
         z16 = [held("z16_%d" % c, [P, n, PACK], BF16) for c, n in enumerate(CHUNKS)]
         z_codes = [held("zc_%d" % c, [P, n], U32) for c, n in enumerate(CHUNKS)]
         z_sc = [held("zs_%d" % c, [P, n], U8) for c, n in enumerate(CHUNKS)]
@@ -199,7 +209,7 @@ def tile_list_ad_auction_bids_kernel(tc, tab_words, tab_scales, offs, w1, pos1, 
         def gather_ad(c, t):
             j0, n = starts[c], CHUNKS[c]
             nc.vector.tensor_tensor(
-                z32[c][:, t, :], h[AD, t][:].indirect(pos1_sb[:, j0 // 16 : (j0 + n) // 16]), gate[:, t, j0 : j0 + n], ALU.mult
+                z32[c][:, t, 0:n], h[AD, t][:].indirect(pos1_sb[:, j0 // 16 : (j0 + n) // 16]), gate[:, t, j0 : j0 + n], ALU.mult
             )
 
         def cast_z(eng, c, n0, n1):
@@ -241,7 +251,6 @@ def tile_list_ad_auction_bids_kernel(tc, tab_words, tab_scales, offs, w1, pos1, 
             nc.sync.dma_start(out=rows.rearrange("(i p) c -> p i c", p=P), in_=bid[:])
 
         cast_w1t("s", CTX, 0, 0, 4)
-
         quant_w1t(CTX, 0, 0, 4)
         gather_tab(0, 0, S)
         gather_sc()
@@ -256,48 +265,36 @@ def tile_list_ad_auction_bids_kernel(tc, tab_words, tab_scales, offs, w1, pos1, 
         for t in range(PACK):
             for ih in range(2):
                 mm1(CTX, t, ih, 1)
-        for t in range(PACK):
-            h_out("s", CTX, t, 0)
-            h_out("v" if t < 0 else "s", CTX, t, 1)
+                h_out("s", CTX, t, ih)
         cast_w1t("v", AD, 0, 0, 4)
-
         quant_w1t(AD, 0, 0, 4)
         cast_w1t("v", AD, 1, 0, 4)
-
-        quant_w1t(AD, 1, 0, 2)
-        quant_w1t(AD, 1, 2, 4)
+        for t in range(PACK):
+            quant_w1t(AD, 1, t, t + 1)
+        for t in range(PACK):
+            gather_ctx(picked, t)
         for t in range(PACK):
             for ih in range(2):
                 mm1(AD, t, ih, 0)
                 mm1(AD, t, ih, 1)
-        for t in range(PACK):
-            gather_ctx(t)
+                h_out("s", AD, t, ih)
             sigmoid_ctx(t)
-            h_out("s", AD, t, 0)
-            h_out("v" if t >= 4 - 0 else "s", AD, t, 1)
-        cast_wv("s", 0, 256)
-        for t in range(PACK):
-            gather_ad(0, t)
-        cast_z("v", 0, 0, 128)
-        cast_z("s", 0, 128, 256)
-        quant_wv(0, 256)
-        quant_z(0)
-        cast_wv("v", 256, 512)
-        cast_wv("v", 512, 768)
-        gather_ad(1, 0)
-        quant_wv(256, 512)
-        gather_ad(1, 1)
-        quant_wv(512, 768)
-        for t in range(2, PACK):
-            gather_ad(1, t)
-        cast_z("v", 1, 0, 256)
-        for u in range(3):
-            s2mm("val", 0, 2*u, 2*u+2)
-            s2mm("clk", 0, 2*u, 2*u+2)
-        quant_z(1)
-        for u in range(3):
-            s2mul(0, 2*u, 2*u+2)
-        for n0, n1 in ((0, 2), (2, 4), (4, 5), (5, 6)):
-            s2mm("val", 1, n0, n1)
-            s2mm("clk", 1, n0, n1)
-            s2mul(1, n0, n1)
+        for u, eng in enumerate("vss"):
+            cast_wv(eng, u)
+        for c, n in enumerate(CHUNKS):
+            for t in range(PACK):
+                gather_ad(c, t)
+            cast_z("v", c, 0, n)
+            quant_z(c)
+            if c == 0:
+                for u in range(3):
+                    quant_wv(u)
+        for c, n in enumerate(CHUNKS):
+            if c == len(CHUNKS) - 1 and n == 256:
+                groups = ((0, 2), (2, 4), (4, 5), (5, 6))
+            else:
+                groups = ((0, 2), (2, 4), (4, 6)) if n == 256 else ((0, 4), (4, 6))
+            for n0, n1 in groups:
+                s2mm("val", c, n0, n1)
+                s2mm("clk", c, n0, n1)
+                s2mul(c, n0, n1)

@@ -41,7 +41,10 @@ def tile_list_ad_auction_bids_kernel(tc, tab_words, tab_scales, offs, w1, pos1, 
 
         tab_sc = held("tab_sc", [P, T // 4], I32)
         wc_sc = held("wc_sc", [P, N // 4], I32)
-        nc.vector.memset(tab_sc[:], 0)
+        nc.vector.memset(tab_sc[32:64, :], 0)
+        nc.vector.memset(tab_sc[64:P, :], 0)
+        planes = held("planes", [P, S // 4], I32)
+        nc.vector.memset(planes[:], 0)
         nc.vector.memset(wc_sc[:], 0)
         warm = held("warm", [P, 16], F32)
         nc.vector.memset(warm[:, 0:8], 0.0)
@@ -65,11 +68,19 @@ def tile_list_ad_auction_bids_kernel(tc, tab_words, tab_scales, offs, w1, pos1, 
         ts32 = tab_scales.bitcast(I32)
         ws32 = wc_scales.bitcast(I32)
 
-        def load_tab_sc(a, r):
-            nc.sync.dma_start(out=tab_sc[4 * a + r : P : 32, :], in_=ts32[a, r:16:4, :])
+        def load_tab_sc():
+            nc.sync.dma_start(out=tab_sc[0:32, :], in_=ts32.rearrange("a q t -> (a q) t"))
 
         def load_wc_sc(q):
             nc.sync.dma_start(out=wc_sc[32 * q : 32 * q + 4, :], in_=ws32[0, 4 * q : 4 * q + 4, :])
+
+        got_sc = held("got_sc", [P, S], U8)
+
+        def gather_sc():
+            nc.vector.tensor_copy(got_sc[:], tab_sc[:].bitcast(U8).indirect(offs_sb[:]))
+
+        def move_sc(a, r):
+            nc.sync.dma_start(out=planes[4 * a + r : P : 32, :], in_=got_sc[:].bitcast(I32)[16 * a + r : 16 * (a + 1) : 4, :])
 
         lists = {"offs": (offs_sb, offs), "pos1": (pos1_sb, pos1), "pos2": (pos2_sb, pos2)}
 
@@ -82,16 +93,16 @@ def tile_list_ad_auction_bids_kernel(tc, tab_words, tab_scales, offs, w1, pos1, 
         def load_wc():
             nc.sync.dma_start(out=wc_codes[:].bitcast(I32), in_=wc_words[0].bitcast(I32))
 
-        load_w1(CTX, 0, 0, H)
+        load_tab_sc()
         load_list("offs")
-        for r in range(2):
-            for a in range(2):
-                load_tab_sc(a, r)
+        load_w1(CTX, 0, 0, H)
         load_tab(0)
-        for r in range(2, 4):
-            for a in range(2):
-                load_tab_sc(a, r)
+        gather_sc()
+        for r in range(4):
+            move_sc(0, r)
         load_tab(1)
+        for r in range(4):
+            move_sc(1, r)
         load_w1(CTX, 1, 0, H)
         load_w1(AD, 0, 0, H)
         load_w1(AD, 1, 0, H)
@@ -137,18 +148,15 @@ def tile_list_ad_auction_bids_kernel(tc, tab_words, tab_scales, offs, w1, pos1, 
             )
 
         got = [held("got%d" % a, [P, S], U32) for a in range(2)]
-        got_sc = held("got_sc", [P, S], U8)
 
         def gather_tab(a, i0, i1):
             nc.vector.tensor_copy(got[a][:, i0:i1], tab[a][:].bitcast(U32).indirect(offs_sb[:, i0 // 16 : i1 // 16]))
 
-        def gather_sc():
-            nc.vector.tensor_copy(got_sc[:], tab_sc[:].bitcast(U8).indirect(offs_sb[:]))
 
         acc = {}
 
-        def mm1(half, t, ih, a):
-            if a == 0:
+        def mm1(half, t, ih, a, first=0):
+            if a == first:
                 acc[half, t, ih] = psum.tile([P, BANK], F32, name="bank")
             cols = slice(BANK * ih, BANK * (ih + 1))
             nc.tensor.matmul_mx(
@@ -156,9 +164,9 @@ def tile_list_ad_auction_bids_kernel(tc, tab_words, tab_scales, offs, w1, pos1, 
                 lhsT=w1_codes[half, a][:, P * t : P * (t + 1)].bitcast(FP8X4),
                 lhsT_scale=w1_sc[half, a][:, P * t : P * (t + 1)],
                 rhs=got[a][:, cols].bitcast(FP8X4),
-                rhs_scale=got_sc[4 * a : P, cols],
-                start=(a == 0),
-                stop=(a == 1),
+                rhs_scale=planes[:].bitcast(U8)[4 * a : P, cols],
+                start=(a == first),
+                stop=(a != first),
             )
 
         h = {}
@@ -253,7 +261,6 @@ def tile_list_ad_auction_bids_kernel(tc, tab_words, tab_scales, offs, w1, pos1, 
         cast_w1t("s", CTX, 0, 0, 4)
         quant_w1t(CTX, 0, 0, 4)
         gather_tab(0, 0, S)
-        gather_sc()
         for t in range(PACK):
             for ih in range(2):
                 mm1(CTX, t, ih, 0)
@@ -275,8 +282,9 @@ def tile_list_ad_auction_bids_kernel(tc, tab_words, tab_scales, offs, w1, pos1, 
             gather_ctx(picked, t)
         for t in range(PACK):
             for ih in range(2):
-                mm1(AD, t, ih, 0)
-                mm1(AD, t, ih, 1)
+                first = 0 if t < 2 else 1
+                mm1(AD, t, ih, first, first)
+                mm1(AD, t, ih, 1 - first, first)
                 h_out("s", AD, t, ih)
             sigmoid_ctx(t)
         for u, eng in enumerate("vss"):

@@ -54,13 +54,16 @@ def tile_list_ad_auction_bids_kernel(tc, tab_words, tab_scales, offs, w1, pos1, 
         raw = {}
         for half in (CTX, AD):
             for a in range(2):
-                raw[half, a] = held("raw%d%d" % (half, a), [P, PACK, H], F32)
+                if (half, a) != (AD, 1):
+                    raw[half, a] = held("raw%d%d" % (half, a), [P, PACK, H], F32)
+        last_raw = [held("last_raw%d" % u, [P, PACK, H // 2], F32) for u in range(2)]
         wv_raw = held("wv_raw", [P, PACK, N], F32)
         wc_codes = held("wc_codes", [P, 2 * N], U8)
 
         def load_w1(half, a, c0, c1):
             rows = w1[KP * a : KP * (a + 1), half * H + c0 : half * H + c1]
-            nc.sync.dma_start(out=raw[half, a][:, :, c0:c1], in_=rows.rearrange("(p j) c -> p j c", j=PACK))
+            dst = last_raw[c0 // (H // 2)][:] if (half, a) == (AD, 1) else raw[half, a][:, :, c0:c1]
+            nc.sync.dma_start(out=dst, in_=rows.rearrange("(p j) c -> p j c", j=PACK))
 
         def load_tab(a):
             nc.sync.dma_start(out=tab[a][:], in_=tab_words[a].rearrange("p n t -> p (n t)").bitcast(I32))
@@ -105,7 +108,8 @@ def tile_list_ad_auction_bids_kernel(tc, tab_words, tab_scales, offs, w1, pos1, 
             move_sc(1, r)
         load_w1(CTX, 1, 0, H)
         load_w1(AD, 0, 0, H)
-        load_w1(AD, 1, 0, H)
+        load_w1(AD, 1, 0, H // 2)
+        load_w1(AD, 1, H // 2, H)
         load_list("pos2")
         load_list("pos1")
         load_wv()
@@ -132,13 +136,14 @@ def tile_list_ad_auction_bids_kernel(tc, tab_words, tab_scales, offs, w1, pos1, 
             else:
                 nc.gpsimd.tensor_scalar(dst, src, 1.0, 0.0, ALU.mult, ALU.add)
 
-        def cast_w1t(eng, half, a, t0, t1):
+        def cast_w1t(eng, half, a, t0, t1, m0=0, m1=P):
             if (half, a) == (AD, 1):
                 dst = late[:, t0:t1, :].rearrange("p t (m j) -> p m j t", j=PACK)
             else:
                 dst = grouped[half, a][:, KP * t0 : KP * t1].rearrange("p (t m j) -> p m j t", m=P, j=PACK)
-            src = raw[half, a][:].rearrange("p j (m t) -> p m j t", t=PACK)[:, :, :, t0:t1]
-            cast(eng, dst, src)
+            rows = last_raw[m0 // (P // 2)] if (half, a) == (AD, 1) else raw[half, a]
+            src = rows[:].rearrange("p j (m t) -> p m j t", t=PACK)[:, :, :, t0:t1]
+            cast(eng, dst[:, m0:m1], src)
 
         def quant_w1t(half, a, t0, t1):
             nc.vector.quantize_mx(
@@ -186,8 +191,8 @@ def tile_list_ad_auction_bids_kernel(tc, tab_words, tab_scales, offs, w1, pos1, 
         def gather_ctx(picked, t):
             nc.vector.tensor_copy(picked[:, t, :], h[CTX, t][:].indirect(pos2_sb[:]))
 
-        def sigmoid_ctx(t):
-            nc.scalar.activation(gate[:, t, :], picked[:, t, :], ACT.Sigmoid)
+        def sigmoid_ctx(t0, t1, j0, j1):
+            nc.scalar.activation(gate[:, t0:t1, j0:j1], picked[:, t0:t1, j0:j1], ACT.Sigmoid)
 
         wv_grp = [held("wv_grp%d" % u, [P, WV_COLS, PACK], BF16) for u in range(N // WV_COLS)]
         wv_codes = held("wv_codes", [P, N], U32)
@@ -209,19 +214,18 @@ def tile_list_ad_auction_bids_kernel(tc, tab_words, tab_scales, offs, w1, pos1, 
             )
 
         starts = [sum(CHUNKS[:c]) for c in range(len(CHUNKS))]
-        z32 = [held("z32", [P, PACK, max(CHUNKS)], F32)] * len(CHUNKS)
+        z32 = held("z32", [P, PACK, PAIRS], F32)
         z16 = [held("z16_%d" % c, [P, n, PACK], BF16) for c, n in enumerate(CHUNKS)]
         z_codes = [held("zc_%d" % c, [P, n], U32) for c, n in enumerate(CHUNKS)]
         z_sc = [held("zs_%d" % c, [P, n], U8) for c, n in enumerate(CHUNKS)]
 
-        def gather_ad(c, t):
-            j0, n = starts[c], CHUNKS[c]
+        def gather_ad(t, j0, j1):
             nc.vector.tensor_tensor(
-                z32[c][:, t, 0:n], h[AD, t][:].indirect(pos1_sb[:, j0 // 16 : (j0 + n) // 16]), gate[:, t, j0 : j0 + n], ALU.mult
+                z32[:, t, j0:j1], h[AD, t][:].indirect(pos1_sb[:, j0 // 16 : j1 // 16]), gate[:, t, j0:j1], ALU.mult
             )
 
         def cast_z(eng, c, n0, n1):
-            cast(eng, z16[c][:, n0:n1, :].rearrange("p (c i) j -> p c j i", i=4), z32[c][:, :, n0:n1].rearrange("p j (c i) -> p c j i", i=4))
+            cast(eng, z16[c][:, n0:n1, :].rearrange("p (c i) j -> p c j i", i=4), z32[:, :, starts[c] + n0 : starts[c] + n1].rearrange("p j (c i) -> p c j i", i=4))
 
         def quant_z(c):
             nc.vector.quantize_mx(
@@ -275,7 +279,8 @@ def tile_list_ad_auction_bids_kernel(tc, tab_words, tab_scales, offs, w1, pos1, 
                 h_out("s", CTX, t, ih)
         cast_w1t("v", AD, 0, 0, 4)
         quant_w1t(AD, 0, 0, 4)
-        cast_w1t("v", AD, 1, 0, 4)
+        cast_w1t("v", AD, 1, 0, 4, 0, 64)
+        cast_w1t("v", AD, 1, 0, 4, 64, 128)
         for t in range(PACK):
             quant_w1t(AD, 1, t, t + 1)
         for t in range(PACK):
@@ -286,17 +291,24 @@ def tile_list_ad_auction_bids_kernel(tc, tab_words, tab_scales, offs, w1, pos1, 
                 mm1(AD, t, ih, first, first)
                 mm1(AD, t, ih, 1 - first, first)
                 h_out("s", AD, t, ih)
-            sigmoid_ctx(t)
-        for u, eng in enumerate("vss"):
-            cast_wv(eng, u)
-        for c, n in enumerate(CHUNKS):
+            sigmoid_ctx(t, t + 1, 0, CHUNKS[0])
+        eng = "gsg"
+        for u in range(2):
+            cast_wv(eng[u], u)
+        sigmoid_ctx(0, PACK, CHUNKS[0], PAIRS)
+        for u in range(2, 3):
+            cast_wv(eng[u], u)
+        for t in range(PACK):
+            gather_ad(t, 0, CHUNKS[0])
+        cast_z("v", 0, 0, CHUNKS[0])
+        quant_z(0)
+        for u in range(3):
+            quant_wv(u)
+        for c in range(1, len(CHUNKS)):
             for t in range(PACK):
-                gather_ad(c, t)
-            cast_z("v", c, 0, n)
+                gather_ad(t, starts[c], starts[c] + CHUNKS[c])
+            cast_z("v", c, 0, CHUNKS[c])
             quant_z(c)
-            if c == 0:
-                for u in range(3):
-                    quant_wv(u)
         for c, n in enumerate(CHUNKS):
             if c == len(CHUNKS) - 1 and n == 256:
                 groups = ((0, 2), (2, 4), (4, 5), (5, 6))

@@ -54,16 +54,13 @@ def tile_list_ad_auction_bids_kernel(tc, tab_words, tab_scales, offs, w1, pos1, 
         raw = {}
         for half in (CTX, AD):
             for a in range(2):
-                if (half, a) != (AD, 1):
-                    raw[half, a] = held("raw%d%d" % (half, a), [P, PACK, H], F32)
-        last_raw = [held("last_raw%d" % u, [P, PACK, H // 2], F32) for u in range(2)]
-        wv_raw = held("wv_raw", [P, PACK, N], F32)
+                raw[half, a] = held("raw%d%d" % (half, a), [P, PACK, H], F32)
+        wv_raw = [held("wv_raw%d" % u, [P, PACK, WV_COLS], F32) for u in range(N // WV_COLS)]
         wc_codes = held("wc_codes", [P, 2 * N], U8)
 
         def load_w1(half, a, c0, c1):
             rows = w1[KP * a : KP * (a + 1), half * H + c0 : half * H + c1]
-            dst = last_raw[c0 // (H // 2)][:] if (half, a) == (AD, 1) else raw[half, a][:, :, c0:c1]
-            nc.sync.dma_start(out=dst, in_=rows.rearrange("(p j) c -> p j c", j=PACK))
+            nc.sync.dma_start(out=raw[half, a][:, :, c0:c1], in_=rows.rearrange("(p j) c -> p j c", j=PACK))
 
         def load_tab(a):
             nc.sync.dma_start(out=tab[a][:], in_=tab_words[a].rearrange("p n t -> p (n t)").bitcast(I32))
@@ -90,8 +87,8 @@ def tile_list_ad_auction_bids_kernel(tc, tab_words, tab_scales, offs, w1, pos1, 
         def load_list(name):
             nc.sync.dma_start(lists[name][0][:], lists[name][1])
 
-        def load_wv(c0=0, c1=N):
-            nc.sync.dma_start(out=wv_raw[:, :, c0:c1], in_=wv[:, c0:c1].rearrange("(p j) c -> p j c", j=PACK))
+        def load_wv(u):
+            nc.sync.dma_start(out=wv_raw[u][:], in_=wv[:, WV_COLS * u : WV_COLS * (u + 1)].rearrange("(p j) c -> p j c", j=PACK))
 
         def load_wc():
             nc.sync.dma_start(out=wc_codes[:].bitcast(I32), in_=wc_words[0].bitcast(I32))
@@ -108,16 +105,18 @@ def tile_list_ad_auction_bids_kernel(tc, tab_words, tab_scales, offs, w1, pos1, 
             move_sc(1, r)
         load_w1(CTX, 1, 0, H)
         load_w1(AD, 0, 0, H)
-        load_w1(AD, 1, 0, H // 2)
-        load_w1(AD, 1, H // 2, H)
+        load_w1(AD, 1, 0, H)
         load_list("pos2")
         load_list("pos1")
-        load_wv()
+        for u in range(N // WV_COLS):
+            load_wv(u)
         load_wc()
         for q in range(4):
             load_wc_sc(q)
 
         grouped, w1_codes, w1_sc = {}, {}, {}
+        wv_grp = [held("wv_grp%d" % u, [P, WV_COLS, PACK], BF16) for u in range(N // WV_COLS)]
+        last = wv_grp[0][:].rearrange("p c j -> p (c j)")[:, 0:KP]
         picked_tile = held("picked", [P, PACK * PAIRS], F32)
         picked = picked_tile[:].rearrange("p (t j) -> p t j", t=PACK)
         late = picked_tile[:].bitcast(BF16).rearrange("p (t x) -> p t x", t=PACK)[:, :, 0:KP]
@@ -136,20 +135,21 @@ def tile_list_ad_auction_bids_kernel(tc, tab_words, tab_scales, offs, w1, pos1, 
             else:
                 nc.gpsimd.tensor_scalar(dst, src, 1.0, 0.0, ALU.mult, ALU.add)
 
-        def cast_w1t(eng, half, a, t0, t1, m0=0, m1=P):
-            if (half, a) == (AD, 1):
+        def cast_w1t(eng, half, a, t0, t1):
+            if (half, a, t0) == (AD, 1, 3):
+                dst = last.rearrange("p (t m j) -> p m j t", t=1, j=PACK)
+            elif (half, a) == (AD, 1):
                 dst = late[:, t0:t1, :].rearrange("p t (m j) -> p m j t", j=PACK)
             else:
                 dst = grouped[half, a][:, KP * t0 : KP * t1].rearrange("p (t m j) -> p m j t", m=P, j=PACK)
-            rows = last_raw[m0 // (P // 2)] if (half, a) == (AD, 1) else raw[half, a]
-            src = rows[:].rearrange("p j (m t) -> p m j t", t=PACK)[:, :, :, t0:t1]
-            cast(eng, dst[:, m0:m1], src)
+            src = raw[half, a][:].rearrange("p j (m t) -> p m j t", t=PACK)[:, :, :, t0:t1]
+            cast(eng, dst, src)
 
         def quant_w1t(half, a, t0, t1):
             nc.vector.quantize_mx(
                 out=w1_codes[half, a][:, P * t0 : P * t1].bitcast(FP8X4),
                 scales=w1_sc[half, a][:, P * t0 : P * t1],
-                in_=late[:, t0, :] if (half, a) == (AD, 1) else grouped[half, a][:, KP * t0 : KP * t1],
+                in_=last if (half, a, t0) == (AD, 1, 3) else late[:, t0, :] if (half, a) == (AD, 1) else grouped[half, a][:, KP * t0 : KP * t1],
             )
 
         got = [held("got%d" % a, [P, S], U32) for a in range(2)]
@@ -194,12 +194,11 @@ def tile_list_ad_auction_bids_kernel(tc, tab_words, tab_scales, offs, w1, pos1, 
         def sigmoid_ctx(t0, t1, j0, j1):
             nc.scalar.activation(gate[:, t0:t1, j0:j1], picked[:, t0:t1, j0:j1], ACT.Sigmoid)
 
-        wv_grp = [held("wv_grp%d" % u, [P, WV_COLS, PACK], BF16) for u in range(N // WV_COLS)]
         wv_codes = held("wv_codes", [P, N], U32)
         wv_sc = held("wv_sc", [P, N], U8)
 
         def cast_wv(eng, u):
-            src = wv_raw[:, :, WV_COLS * u : WV_COLS * (u + 1)]
+            src = wv_raw[u][:]
             if eng == "g":
                 cast(eng, wv_grp[u][:], src.rearrange("p j c -> p c j"))
             else:
@@ -279,8 +278,8 @@ def tile_list_ad_auction_bids_kernel(tc, tab_words, tab_scales, offs, w1, pos1, 
                 h_out("s", CTX, t, ih)
         cast_w1t("v", AD, 0, 0, 4)
         quant_w1t(AD, 0, 0, 4)
-        cast_w1t("v", AD, 1, 0, 4, 0, 64)
-        cast_w1t("v", AD, 1, 0, 4, 64, 128)
+        cast_w1t("v", AD, 1, 0, 3)
+        cast_w1t("v", AD, 1, 3, 4)
         for t in range(PACK):
             quant_w1t(AD, 1, t, t + 1)
         for t in range(PACK):
@@ -292,11 +291,11 @@ def tile_list_ad_auction_bids_kernel(tc, tab_words, tab_scales, offs, w1, pos1, 
                 mm1(AD, t, ih, 1 - first, first)
                 h_out("s", AD, t, ih)
             sigmoid_ctx(t, t + 1, 0, CHUNKS[0])
-        eng = "gsg"
-        for u in range(2):
+        eng = "ggs"
+        for u in range(3):
             cast_wv(eng[u], u)
         sigmoid_ctx(0, PACK, CHUNKS[0], PAIRS)
-        for u in range(2, 3):
+        for u in range(3, 3):
             cast_wv(eng[u], u)
         for t in range(PACK):
             gather_ad(t, 0, CHUNKS[0])

@@ -54,13 +54,16 @@ def tile_list_ad_auction_bids_kernel(tc, tab_words, tab_scales, offs, w1, pos1, 
         raw = {}
         for half in (CTX, AD):
             for a in range(2):
-                raw[half, a] = held("raw%d%d" % (half, a), [P, PACK, H], F32)
+                if (half, a) != (AD, 1):
+                    raw[half, a] = held("raw%d%d" % (half, a), [P, PACK, H], F32)
+        last_raw = [held("last_raw%d" % u, [P, PACK, H // 2], F32) for u in range(2)]
         wv_raw = [held("wv_raw%d" % u, [P, PACK, WV_COLS], F32) for u in range(N // WV_COLS)]
         wc_codes = held("wc_codes", [P, 2 * N], U8)
 
         def load_w1(half, a, c0, c1):
             rows = w1[KP * a : KP * (a + 1), half * H + c0 : half * H + c1]
-            nc.sync.dma_start(out=raw[half, a][:, :, c0:c1], in_=rows.rearrange("(p j) c -> p j c", j=PACK))
+            dst = last_raw[c0 // (H // 2)][:] if (half, a) == (AD, 1) else raw[half, a][:, :, c0:c1]
+            nc.sync.dma_start(out=dst, in_=rows.rearrange("(p j) c -> p j c", j=PACK))
 
         def load_tab(a):
             nc.sync.dma_start(out=tab[a][:], in_=tab_words[a].rearrange("p n t -> p (n t)").bitcast(I32))
@@ -105,21 +108,21 @@ def tile_list_ad_auction_bids_kernel(tc, tab_words, tab_scales, offs, w1, pos1, 
             move_sc(1, r)
         load_w1(CTX, 1, 0, H)
         load_w1(AD, 0, 0, H)
-        load_w1(AD, 1, 0, H)
-        load_list("pos2")
+        load_w1(AD, 1, 0, H // 2)
+        load_w1(AD, 1, H // 2, H)
         load_list("pos1")
-        for u in range(N // WV_COLS):
-            load_wv(u)
+        load_wv(0)
+        load_list("pos2")
+        load_wv(1)
+        load_wv(2)
         load_wc()
         for q in range(4):
             load_wc_sc(q)
 
         grouped, w1_codes, w1_sc = {}, {}, {}
-        wv_grp = [held("wv_grp%d" % u, [P, WV_COLS, PACK], BF16) for u in range(N // WV_COLS)]
-        last = wv_grp[0][:].rearrange("p c j -> p (c j)")[:, 0:KP]
-        picked_tile = held("picked", [P, PACK * PAIRS], F32)
-        picked = picked_tile[:].rearrange("p (t j) -> p t j", t=PACK)
-        late = picked_tile[:].bitcast(BF16).rearrange("p (t x) -> p t x", t=PACK)[:, :, 0:KP]
+        shared = held("shared", [P, (PACK + 1) * PAIRS], F32)
+        picked = shared[:, 0 : PACK * PAIRS].rearrange("p (t j) -> p t j", t=PACK)
+        late = shared[:, PAIRS:].bitcast(BF16).rearrange("p (t x) -> p t x", t=PACK)[:, :, 0:KP]
         for half in (CTX, AD):
             for a in range(2):
                 if (half, a) != (AD, 1):
@@ -135,21 +138,20 @@ def tile_list_ad_auction_bids_kernel(tc, tab_words, tab_scales, offs, w1, pos1, 
             else:
                 nc.gpsimd.tensor_scalar(dst, src, 1.0, 0.0, ALU.mult, ALU.add)
 
-        def cast_w1t(eng, half, a, t0, t1):
-            if (half, a, t0) == (AD, 1, 3):
-                dst = last.rearrange("p (t m j) -> p m j t", t=1, j=PACK)
-            elif (half, a) == (AD, 1):
+        def cast_w1t(eng, half, a, t0, t1, m0=0, m1=P):
+            if (half, a) == (AD, 1):
                 dst = late[:, t0:t1, :].rearrange("p t (m j) -> p m j t", j=PACK)
             else:
                 dst = grouped[half, a][:, KP * t0 : KP * t1].rearrange("p (t m j) -> p m j t", m=P, j=PACK)
-            src = raw[half, a][:].rearrange("p j (m t) -> p m j t", t=PACK)[:, :, :, t0:t1]
-            cast(eng, dst, src)
+            rows = last_raw[m0 // (P // 2)] if (half, a) == (AD, 1) else raw[half, a]
+            src = rows[:].rearrange("p j (m t) -> p m j t", t=PACK)[:, :, :, t0:t1]
+            cast(eng, dst[:, m0:m1], src)
 
         def quant_w1t(half, a, t0, t1):
             nc.vector.quantize_mx(
                 out=w1_codes[half, a][:, P * t0 : P * t1].bitcast(FP8X4),
                 scales=w1_sc[half, a][:, P * t0 : P * t1],
-                in_=last if (half, a, t0) == (AD, 1, 3) else late[:, t0, :] if (half, a) == (AD, 1) else grouped[half, a][:, KP * t0 : KP * t1],
+                in_=late[:, t0, :] if (half, a) == (AD, 1) else grouped[half, a][:, KP * t0 : KP * t1],
             )
 
         got = [held("got%d" % a, [P, S], U32) for a in range(2)]
@@ -194,6 +196,8 @@ def tile_list_ad_auction_bids_kernel(tc, tab_words, tab_scales, offs, w1, pos1, 
         def sigmoid_ctx(t0, t1, j0, j1):
             nc.scalar.activation(gate[:, t0:t1, j0:j1], picked[:, t0:t1, j0:j1], ACT.Sigmoid)
 
+        wv_grp = [shared[:, PACK * PAIRS :].bitcast(BF16).rearrange("p (c j) -> p c j", j=PACK)]
+        wv_grp.extend(held("wv_grp%d" % u, [P, WV_COLS, PACK], BF16)[:] for u in range(1, N // WV_COLS))
         wv_codes = held("wv_codes", [P, N], U32)
         wv_sc = held("wv_sc", [P, N], U8)
 
@@ -278,8 +282,8 @@ def tile_list_ad_auction_bids_kernel(tc, tab_words, tab_scales, offs, w1, pos1, 
                 h_out("s", CTX, t, ih)
         cast_w1t("v", AD, 0, 0, 4)
         quant_w1t(AD, 0, 0, 4)
-        cast_w1t("v", AD, 1, 0, 3)
-        cast_w1t("v", AD, 1, 3, 4)
+        cast_w1t("v", AD, 1, 0, 4, 0, 64)
+        cast_w1t("v", AD, 1, 0, 4, 64, 128)
         for t in range(PACK):
             quant_w1t(AD, 1, t, t + 1)
         for t in range(PACK):

@@ -22,7 +22,7 @@ KP = 512
 BANK = 512
 LN_HALF = -0.6931471805599453
 CTX, AD = 1, 0
-CHUNKS = [256, 128, 128]
+CHUNKS = [256, 256]
 WV_COLS = 256
 
 

@@ -22,8 +22,10 @@ KP = 512
 BANK = 512
 LN_HALF = -0.6931471805599453
 CTX, AD = 1, 0
-CHUNKS = [256, 256]
+CHUNKS = [256, 128, 128]
 WV_COLS = 256
+FIRST = 256
+Z16TAG = ["za", "zb", "zc", "zd"]
 
 
 def tile_list_ad_auction_bids_kernel(tc, tab_words, tab_scales, offs, w1, pos1, pos2, wc_words, wc_scales, wv, out):
@@ -32,8 +34,8 @@ def tile_list_ad_auction_bids_kernel(tc, tab_words, tab_scales, offs, w1, pos1, 
         keep = ctx.enter_context(tc.tile_pool(name="keep", bufs=1))
         psum = ctx.enter_context(tc.psum_pool(name="psum", bufs=8))
 
-        def held(name, shape, dtype):
-            return keep.tile(shape, dtype, name=name, align_bytes=64)
+        def held(name, shape, dtype, tag=None):
+            return keep.tile(shape, dtype, name=name, tag=tag or name, align_bytes=64)
 
         offs_sb = keep.tile([P, S // 16], U16, name="offs_sb")
         pos1_sb = keep.tile([P, PAIRS // 16], U16, name="pos1_sb")
@@ -188,25 +190,33 @@ def tile_list_ad_auction_bids_kernel(tc, tab_words, tab_scales, offs, w1, pos1, 
             else:
                 nc.scalar.copy(out=dst, in_=acc[half, t, ih][:])
 
-        gate = held("gate", [P, PACK, PAIRS], F32)
+        gate_row = held("gate", [P, PACK * PAIRS], F32)
+        gate = gate_row[:].rearrange("p (t j) -> p t j", t=PACK)
 
-        def gather_ctx(picked, t):
-            nc.vector.tensor_copy(picked[:, t, :], h[CTX, t][:].indirect(pos2_sb[:]))
+        def slot(t):
+            return (t + 1) % PACK
 
-        def sigmoid_ctx(t0, t1, j0, j1):
-            nc.scalar.activation(gate[:, t0:t1, j0:j1], picked[:, t0:t1, j0:j1], ACT.Sigmoid)
+        def gather_ctx(t, j0, j1):
+            nc.vector.tensor_copy(picked[:, slot(t), j0:j1], h[CTX, t][:].indirect(pos2_sb[:, j0 // 16 : j1 // 16]))
+
+        def sigmoid_first(t):
+            nc.scalar.activation(gate[:, slot(t), 0:FIRST], picked[:, slot(t), 0:FIRST], ACT.Sigmoid)
+
+        def sigmoid_rest(j0, j1):
+            nc.scalar.activation(gate[:, :, j0:j1], picked[:, :, j0:j1], ACT.Sigmoid)
 
         wv_grp = [shared[:, PACK * PAIRS :].bitcast(BF16).rearrange("p (c j) -> p c j", j=PACK)]
         wv_grp.extend(held("wv_grp%d" % u, [P, WV_COLS, PACK], BF16)[:] for u in range(1, N // WV_COLS))
         wv_codes = held("wv_codes", [P, N], U32)
         wv_sc = held("wv_sc", [P, N], U8)
 
-        def cast_wv(eng, u):
-            src = wv_raw[u][:]
+        def cast_wv(eng, u, c0=0, c1=WV_COLS):
+            src = wv_raw[u][:, :, c0:c1]
+            dst = wv_grp[u][:, c0:c1, :]
             if eng == "g":
-                cast(eng, wv_grp[u][:], src.rearrange("p j c -> p c j"))
+                cast(eng, dst, src.rearrange("p j c -> p c j"))
             else:
-                cast(eng, wv_grp[u][:].rearrange("p (c i) j -> p c j i", i=4), src.rearrange("p j (c i) -> p c j i", i=4))
+                cast(eng, dst.rearrange("p (c i) j -> p c j i", i=4), src.rearrange("p j (c i) -> p c j i", i=4))
 
         def quant_wv(u):
             c0, c1 = WV_COLS * u, WV_COLS * (u + 1)
@@ -218,13 +228,13 @@ def tile_list_ad_auction_bids_kernel(tc, tab_words, tab_scales, offs, w1, pos1, 
 
         starts = [sum(CHUNKS[:c]) for c in range(len(CHUNKS))]
         z32 = held("z32", [P, PACK, PAIRS], F32)
-        z16 = [held("z16_%d" % c, [P, n, PACK], BF16) for c, n in enumerate(CHUNKS)]
+        z16 = [held("z16_%d" % c, [P, n, PACK], BF16, Z16TAG[c]) for c, n in enumerate(CHUNKS)]
         z_codes = [held("zc_%d" % c, [P, n], U32) for c, n in enumerate(CHUNKS)]
         z_sc = [held("zs_%d" % c, [P, n], U8) for c, n in enumerate(CHUNKS)]
 
         def gather_ad(t, j0, j1):
             nc.vector.tensor_tensor(
-                z32[:, t, j0:j1], h[AD, t][:].indirect(pos1_sb[:, j0 // 16 : j1 // 16]), gate[:, t, j0:j1], ALU.mult
+                z32[:, t, j0:j1], h[AD, t][:].indirect(pos1_sb[:, j0 // 16 : j1 // 16]), gate[:, slot(t), j0:j1], ALU.mult
             )
 
         def cast_z(eng, c, n0, n1):
@@ -237,10 +247,20 @@ def tile_list_ad_auction_bids_kernel(tc, tab_words, tab_scales, offs, w1, pos1, 
 
         wc_sc8 = wc_sc[:].bitcast(U8)
 
-        acts = {}
+        HALF = 256
+        act = {}
+        bid = {}
+        for g in range(2):
+            for kind in ("val", "clk"):
+                act[kind, g] = held("act_%s%d" % (kind, g), [P, N // P, HALF], F32)
+            bid[g] = held("bid%d" % g, [P, N // P, HALF], F32)
 
-        def s2mm(kind, c, n0, n1):
+        half_word = z32[:, PACK - 1, PAIRS - 1 : PAIRS]
+        nc.vector.memset(half_word, 0.5)
+
+        def s2mm(kind, c, n0, n1, scale=0.5):
             n = CHUNKS[c]
+            g, o = divmod(starts[c], HALF)
             bank = psum.tile([P, n1 - n0, n], F32, name="bank")
             for m in range(n0, n1):
                 cols = slice(P * m, P * (m + 1))
@@ -252,18 +272,25 @@ def tile_list_ad_auction_bids_kernel(tc, tab_words, tab_scales, offs, w1, pos1, 
                     out=bank[:, m - n0, :], lhsT=codes, lhsT_scale=scales,
                     rhs=z_codes[c][:].bitcast(FP8X4), rhs_scale=z_sc[c][:], start=True, stop=True,
                 )
-            acts[kind, c, n0] = held("act_%s%d%d" % (kind, c, n0), [P, n1 - n0, n], F32)
+            dst = act[kind, g][:, n0:n1, o : o + n]
             if kind == "val":
-                nc.scalar.activation(acts[kind, c, n0][:], bank[:], ACT.Exp, bias=LN_HALF)
+                nc.scalar.activation(dst, bank[:], ACT.Exp, bias=LN_HALF)
             else:
-                nc.scalar.activation(acts[kind, c, n0][:], bank[:], ACT.Tanh, scale=0.5)
+                nc.scalar.activation(dst, bank[:], ACT.Tanh, scale=scale)
 
-        def s2mul(c, n0, n1):
-            j0, n = starts[c], CHUNKS[c]
-            bid = held("bid%d%d" % (c, n0), [P, n1 - n0, n], F32)
-            nc.vector.scalar_tensor_tensor(bid[:], acts["clk", c, n0][:], 1.0, acts["val", c, n0][:], ALU.add, ALU.mult)
-            rows = out[P * n0 : P * n1, j0 : j0 + n]
-            nc.sync.dma_start(out=rows.rearrange("(i p) c -> p i c", p=P), in_=bid[:])
+        def mul(n0, n1, j0, j1):
+            g, o = divmod(j0, HALF)
+            w = slice(o, o + j1 - j0)
+            nc.vector.scalar_tensor_tensor(bid[g][:, n0:n1, w], act["clk", g][:, n0:n1, w], 1.0, act["val", g][:, n0:n1, w], ALU.add, ALU.mult)
+
+        def store(n0, n1, j0, j1):
+            g, o = divmod(j0, HALF)
+            rows = out[P * n0 : P * n1, j0:j1]
+            nc.sync.dma_start(out=rows.rearrange("(i p) c -> p i c", p=P), in_=bid[g][:, n0:n1, o : o + j1 - j0])
+
+        def ms(n0, n1, j0, j1):
+            mul(n0, n1, j0, j1)
+            store(n0, n1, j0, j1)
 
         cast_w1t("s", CTX, 0, 0, 4)
         quant_w1t(CTX, 0, 0, 4)
@@ -287,37 +314,64 @@ def tile_list_ad_auction_bids_kernel(tc, tab_words, tab_scales, offs, w1, pos1, 
         for t in range(PACK):
             quant_w1t(AD, 1, t, t + 1)
         for t in range(PACK):
-            gather_ctx(picked, t)
+            gather_ctx(t, 0, PAIRS)
         for t in range(PACK):
             for ih in range(2):
                 first = 0 if t < 2 else 1
                 mm1(AD, t, ih, first, first)
                 mm1(AD, t, ih, 1 - first, first)
                 h_out("s", AD, t, ih)
-            sigmoid_ctx(t, t + 1, 0, CHUNKS[0])
-        eng = "ggs"
-        for u in range(3):
-            cast_wv(eng[u], u)
-        sigmoid_ctx(0, PACK, CHUNKS[0], PAIRS)
-        for u in range(3, 3):
-            cast_wv(eng[u], u)
+            sigmoid_first(t)
+        cast_wv("g", 0, 0, 208)
+        cast_wv("g", 1, 0, 208)
+        cast_wv("g", 2, 0, 224)
+        cast_wv("s", 0, 208, WV_COLS)
+        sigmoid_rest(256, 384)
+        cast_wv("s", 1, 208, WV_COLS)
+        sigmoid_rest(384, 512)
+        cast_wv("s", 2, 224, WV_COLS)
         for t in range(PACK):
-            gather_ad(t, 0, CHUNKS[0])
-        cast_z("v", 0, 0, CHUNKS[0])
+            gather_ad(t, starts[0], starts[0] + CHUNKS[0])
+        cast_z("v", 0, 0, 256)
         quant_z(0)
-        for u in range(3):
-            quant_wv(u)
-        for c in range(1, len(CHUNKS)):
-            for t in range(PACK):
-                gather_ad(t, starts[c], starts[c] + CHUNKS[c])
-            cast_z("v", c, 0, CHUNKS[c])
-            quant_z(c)
-        for c, n in enumerate(CHUNKS):
-            if c == len(CHUNKS) - 1 and n == 256:
-                groups = ((0, 2), (2, 4), (4, 5), (5, 6))
-            else:
-                groups = ((0, 2), (2, 4), (4, 6)) if n == 256 else ((0, 4), (4, 6))
-            for n0, n1 in groups:
-                s2mm("val", c, n0, n1)
-                s2mm("clk", c, n0, n1)
-                s2mul(c, n0, n1)
+        quant_wv(0)
+        quant_wv(1)
+        s2mm("val", 0, 0, 1)
+        s2mm("clk", 0, 0, 1)
+        s2mm("val", 0, 1, 2)
+        s2mm("clk", 0, 1, 2, half_word)
+        s2mm("val", 0, 2, 4)
+        s2mm("clk", 0, 2, 4)
+        for t in range(PACK):
+            gather_ad(t, starts[1], starts[1] + CHUNKS[1])
+        cast_z("v", 1, 0, 128)
+        quant_z(1)
+        quant_wv(2)
+        s2mm("val", 0, 4, 6)
+        s2mm("clk", 0, 4, 6)
+        s2mm("val", 1, 0, 4)
+        s2mm("clk", 1, 0, 4)
+        s2mm("val", 1, 4, 6)
+        s2mm("clk", 1, 4, 6)
+        ms(0, 2, 0, 256)
+        for t in range(PACK):
+            gather_ad(t, starts[2], starts[2] + CHUNKS[2])
+        cast_z("v", 2, 0, 128)
+        quant_z(2)
+        mul(2, 3, 0, 256)
+        mul(3, 4, 0, 256)
+        store(2, 4, 0, 256)
+        ms(4, 6, 0, 256)
+        s2mm("val", 2, 0, 2)
+        s2mm("clk", 2, 0, 2)
+        s2mm("val", 2, 2, 4)
+        s2mm("clk", 2, 2, 4)
+        s2mm("val", 2, 4, 6)
+        s2mm("clk", 2, 4, 6)
+        mul(0,4,256,384)
+        ms(4,6,256,384)
+        mul(0,2,384,512)
+        store(0,2,256,512)
+        mul(2,4,384,512)
+        store(2,4,256,512)
+        ms(4,6,384,512)

@@ -322,14 +322,13 @@ def tile_list_ad_auction_bids_kernel(tc, tab_words, tab_scales, offs, w1, pos1, 
                 mm1(AD, t, ih, 1 - first, first)
                 h_out("s", AD, t, ih)
             sigmoid_first(t)
-        cast_wv("g", 0, 0, 208)
-        cast_wv("g", 1, 0, 208)
-        cast_wv("g", 2, 0, 224)
-        cast_wv("s", 0, 208, WV_COLS)
+        cast_wv("g", 0, 0, 224)
+        cast_wv("g", 1, 0, 224)
+        cast_wv("s", 0, 224, WV_COLS)
         sigmoid_rest(256, 384)
-        cast_wv("s", 1, 208, WV_COLS)
+        cast_wv("s", 1, 224, WV_COLS)
         sigmoid_rest(384, 512)
-        cast_wv("s", 2, 224, WV_COLS)
+        cast_wv("s", 2, 0, WV_COLS)
         for t in range(PACK):
             gather_ad(t, starts[0], starts[0] + CHUNKS[0])
         cast_z("v", 0, 0, 256)

@@ -22,7 +22,7 @@ KP = 512
 BANK = 512
 LN_HALF = -0.6931471805599453
 CTX, AD = 1, 0
-CHUNKS = [256, 128, 128]
+CHUNKS = [256, 256]
 WV_COLS = 256
 FIRST = 256
 Z16TAG = ["za", "zb", "zc", "zd"]
@@ -43,8 +43,7 @@ def tile_list_ad_auction_bids_kernel(tc, tab_words, tab_scales, offs, w1, pos1, 
 
         tab_sc = held("tab_sc", [P, T // 4], I32)
         wc_sc = held("wc_sc", [P, N // 4], I32)
-        nc.vector.memset(tab_sc[32:64, :], 0)
-        nc.vector.memset(tab_sc[64:P, :], 0)
+        nc.vector.memset(tab_sc[:], 0)
         planes = held("planes", [P, S // 4], I32)
         nc.vector.memset(planes[:], 0)
         nc.vector.memset(wc_sc[:], 0)
@@ -74,7 +73,7 @@ def tile_list_ad_auction_bids_kernel(tc, tab_words, tab_scales, offs, w1, pos1, 
         ws32 = wc_scales.bitcast(I32)
 
         def load_tab_sc():
-            nc.sync.dma_start(out=tab_sc[0:32, :], in_=ts32.rearrange("a q t -> (a q) t"))
+            nc.sync.dma_start(out=tab_sc[0:P:4, :], in_=ts32.rearrange("a q t -> (a q) t"))
 
         def load_wc_sc(q):
             nc.sync.dma_start(out=wc_sc[32 * q : 32 * q + 4, :], in_=ws32[0, 4 * q : 4 * q + 4, :])
@@ -85,7 +84,7 @@ def tile_list_ad_auction_bids_kernel(tc, tab_words, tab_scales, offs, w1, pos1, 
             nc.vector.tensor_copy(got_sc[:], tab_sc[:].bitcast(U8).indirect(offs_sb[:]))
 
         def move_sc(a, r):
-            nc.sync.dma_start(out=planes[4 * a + r : P : 32, :], in_=got_sc[:].bitcast(I32)[16 * a + r : 16 * (a + 1) : 4, :])
+            nc.sync.dma_start(out=planes[4 * a + r : P : 32, :], in_=got_sc[:].bitcast(I32)[64 * a + 4 * r : 64 * (a + 1) : 16, :])
 
         lists = {"offs": (offs_sb, offs), "pos1": (pos1_sb, pos1), "pos2": (pos2_sb, pos2)}
 
@@ -98,9 +97,11 @@ def tile_list_ad_auction_bids_kernel(tc, tab_words, tab_scales, offs, w1, pos1, 
         def load_wc():
             nc.sync.dma_start(out=wc_codes[:].bitcast(I32), in_=wc_words[0].bitcast(I32))
 
-        load_tab_sc()
+        rows0 = w1[0:KP, CTX * H : (CTX + 1) * H].rearrange("(p j) c -> p j c", j=PACK)
+        nc.sync.dma_start(out=raw[CTX, 0][:, 0:2, :], in_=rows0[:, 0:2, :])
         load_list("offs")
-        load_w1(CTX, 0, 0, H)
+        load_tab_sc()
+        nc.sync.dma_start(out=raw[CTX, 0][:, 2:4, :], in_=rows0[:, 2:4, :])
         load_tab(0)
         gather_sc()
         for r in range(4):
@@ -202,8 +203,8 @@ def tile_list_ad_auction_bids_kernel(tc, tab_words, tab_scales, offs, w1, pos1, 
         def sigmoid_first(t):
             nc.scalar.activation(gate[:, slot(t), 0:FIRST], picked[:, slot(t), 0:FIRST], ACT.Sigmoid)
 
-        def sigmoid_rest(j0, j1):
-            nc.scalar.activation(gate[:, :, j0:j1], picked[:, :, j0:j1], ACT.Sigmoid)
+        def sigmoid_rest(s0, s1):
+            nc.scalar.activation(gate[:, s0:s1, FIRST:], picked[:, s0:s1, FIRST:], ACT.Sigmoid)
 
         wv_grp = [shared[:, PACK * PAIRS :].bitcast(BF16).rearrange("p (c j) -> p c j", j=PACK)]
         wv_grp.extend(held("wv_grp%d" % u, [P, WV_COLS, PACK], BF16)[:] for u in range(1, N // WV_COLS))
@@ -254,9 +255,6 @@ def tile_list_ad_auction_bids_kernel(tc, tab_words, tab_scales, offs, w1, pos1, 
             for kind in ("val", "clk"):
                 act[kind, g] = held("act_%s%d" % (kind, g), [P, N // P, HALF], F32)
             bid[g] = held("bid%d" % g, [P, N // P, HALF], F32)
-
-        half_word = z32[:, PACK - 1, PAIRS - 1 : PAIRS]
-        nc.vector.memset(half_word, 0.5)
 
         def s2mm(kind, c, n0, n1, scale=0.5):
             n = CHUNKS[c]
@@ -322,55 +320,43 @@ def tile_list_ad_auction_bids_kernel(tc, tab_words, tab_scales, offs, w1, pos1, 
                 mm1(AD, t, ih, 1 - first, first)
                 h_out("s", AD, t, ih)
             sigmoid_first(t)
-        cast_wv("g", 0, 0, 224)
-        cast_wv("g", 1, 0, 224)
-        cast_wv("s", 0, 224, WV_COLS)
-        sigmoid_rest(256, 384)
-        cast_wv("s", 1, 224, WV_COLS)
-        sigmoid_rest(384, 512)
-        cast_wv("s", 2, 0, WV_COLS)
+        cast_wv("g", 0, 0, 240)
+        cast_wv("g", 1, 0, 240)
+        cast_wv("s", 0, 240, WV_COLS)
+        sigmoid_rest(1, 3)
+        cast_wv("s", 1, 240, WV_COLS)
+        sigmoid_rest(3, 4)
+        sigmoid_rest(0, 1)
+        cast_wv("s", 2)
         for t in range(PACK):
             gather_ad(t, starts[0], starts[0] + CHUNKS[0])
         cast_z("v", 0, 0, 256)
         quant_z(0)
         quant_wv(0)
         quant_wv(1)
-        s2mm("val", 0, 0, 1)
-        s2mm("clk", 0, 0, 1)
-        s2mm("val", 0, 1, 2)
-        s2mm("clk", 0, 1, 2, half_word)
+        s2mm("val", 0, 0, 2)
+        s2mm("clk", 0, 0, 2)
         s2mm("val", 0, 2, 4)
         s2mm("clk", 0, 2, 4)
         for t in range(PACK):
             gather_ad(t, starts[1], starts[1] + CHUNKS[1])
-        cast_z("v", 1, 0, 128)
+        cast_z("v", 1, 0, 256)
         quant_z(1)
         quant_wv(2)
-        s2mm("val", 0, 4, 6)
         s2mm("clk", 0, 4, 6)
-        s2mm("val", 1, 0, 4)
-        s2mm("clk", 1, 0, 4)
-        s2mm("val", 1, 4, 6)
-        s2mm("clk", 1, 4, 6)
+        s2mm("val", 0, 4, 6)
         ms(0, 2, 0, 256)
-        for t in range(PACK):
-            gather_ad(t, starts[2], starts[2] + CHUNKS[2])
-        cast_z("v", 2, 0, 128)
-        quant_z(2)
-        mul(2, 3, 0, 256)
-        mul(3, 4, 0, 256)
-        store(2, 4, 0, 256)
+        ms(2, 4, 0, 256)
         ms(4, 6, 0, 256)
-        s2mm("val", 2, 0, 2)
-        s2mm("clk", 2, 0, 2)
-        s2mm("val", 2, 2, 4)
-        s2mm("clk", 2, 2, 4)
-        s2mm("val", 2, 4, 6)
-        s2mm("clk", 2, 4, 6)
-        mul(0,4,256,384)
-        ms(4,6,256,384)
-        mul(0,2,384,512)
-        store(0,2,256,512)
-        mul(2,4,384,512)
-        store(2,4,256,512)
-        ms(4,6,384,512)
+        s2mm("val", 1, 0, 2)
+        s2mm("clk", 1, 0, 2)
+        ms(0, 2, 256, 512)
+        s2mm("val", 1, 2, 4)
+        s2mm("clk", 1, 2, 4)
+        ms(2, 4, 256, 512)
+        s2mm("val", 1, 4, 5)
+        s2mm("clk", 1, 4, 5)
+        ms(4, 5, 256, 512)
+        s2mm("val", 1, 5, 6)
+        s2mm("clk", 1, 5, 6)
+        ms(5, 6, 256, 512)

@@ -25,6 +25,7 @@ CTX, AD = 1, 0
 CHUNKS = [256, 256]
 WV_COLS = 256
 FIRST = 256
+HALF = 256
 Z16TAG = ["za", "zb", "zc", "zd"]
 
 
@@ -241,14 +242,13 @@ def tile_list_ad_auction_bids_kernel(tc, tab_words, tab_scales, offs, w1, pos1, 
         def cast_z(eng, c, n0, n1):
             cast(eng, z16[c][:, n0:n1, :].rearrange("p (c i) j -> p c j i", i=4), z32[:, :, starts[c] + n0 : starts[c] + n1].rearrange("p j (c i) -> p c j i", i=4))
 
-        def quant_z(c):
+        def quant_z(c, n0=0, n1=HALF):
             nc.vector.quantize_mx(
-                out=z_codes[c][:].bitcast(FP8X4), scales=z_sc[c][:], in_=z16[c][:].rearrange("p n t -> p (n t)")
+                out=z_codes[c][:, n0:n1].bitcast(FP8X4), scales=z_sc[c][:, n0:n1], in_=z16[c][:, n0:n1, :].rearrange("p n t -> p (n t)")
             )
 
         wc_sc8 = wc_sc[:].bitcast(U8)
 
-        HALF = 256
         act = {}
         bid = {}
         for g in range(2):
@@ -256,10 +256,8 @@ def tile_list_ad_auction_bids_kernel(tc, tab_words, tab_scales, offs, w1, pos1, 
                 act[kind, g] = held("act_%s%d" % (kind, g), [P, N // P, HALF], F32)
             bid[g] = held("bid%d" % g, [P, N // P, HALF], F32)
 
-        def s2mm(kind, c, n0, n1, scale=0.5):
-            n = CHUNKS[c]
-            g, o = divmod(starts[c], HALF)
-            bank = psum.tile([P, n1 - n0, n], F32, name="bank")
+        def s2mm(kind, c, n0, n1, j0=0, j1=HALF):
+            bank = psum.tile([P, n1 - n0, j1 - j0], F32, name="bank")
             for m in range(n0, n1):
                 cols = slice(P * m, P * (m + 1))
                 if kind == "val":
@@ -268,13 +266,13 @@ def tile_list_ad_auction_bids_kernel(tc, tab_words, tab_scales, offs, w1, pos1, 
                     codes, scales = wc_codes[:, 2 * cols.start : 2 * cols.stop].bitcast(FP4X4), wc_sc8[:, cols]
                 nc.tensor.matmul_mx(
                     out=bank[:, m - n0, :], lhsT=codes, lhsT_scale=scales,
-                    rhs=z_codes[c][:].bitcast(FP8X4), rhs_scale=z_sc[c][:], start=True, stop=True,
+                    rhs=z_codes[c][:, j0:j1].bitcast(FP8X4), rhs_scale=z_sc[c][:, j0:j1], start=True, stop=True,
                 )
-            dst = act[kind, g][:, n0:n1, o : o + n]
+            dst = act[kind, c][:, n0:n1, j0:j1]
             if kind == "val":
                 nc.scalar.activation(dst, bank[:], ACT.Exp, bias=LN_HALF)
             else:
-                nc.scalar.activation(dst, bank[:], ACT.Tanh, scale=scale)
+                nc.scalar.activation(dst, bank[:], ACT.Tanh, scale=0.5)
 
         def mul(n0, n1, j0, j1):
             g, o = divmod(j0, HALF)
@@ -340,15 +338,18 @@ def tile_list_ad_auction_bids_kernel(tc, tab_words, tab_scales, offs, w1, pos1, 
         s2mm("clk", 0, 2, 4)
         for t in range(PACK):
             gather_ad(t, starts[1], starts[1] + CHUNKS[1])
-        cast_z("v", 1, 0, 256)
-        quant_z(1)
+        cast_z("v", 1, 0, 128)
+        cast_z("v", 1, 128, 256)
+        quant_z(1, 0, 128)
+        quant_z(1, 128, 256)
         quant_wv(2)
         s2mm("clk", 0, 4, 6)
         s2mm("val", 0, 4, 6)
         ms(0, 2, 0, 256)
         ms(2, 4, 0, 256)
         ms(4, 6, 0, 256)
-        s2mm("val", 1, 0, 2)
+        s2mm("val", 1, 0, 2, 0, 128)
+        s2mm("val", 1, 0, 2, 128, 256)
         s2mm("clk", 1, 0, 2)
         ms(0, 2, 256, 512)
         s2mm("val", 1, 2, 4)

@@ -208,7 +208,8 @@ def tile_list_ad_auction_bids_kernel(tc, tab_words, tab_scales, offs, w1, pos1, 
             nc.scalar.activation(gate[:, s0:s1, FIRST:], picked[:, s0:s1, FIRST:], ACT.Sigmoid)
 
         wv_grp = [shared[:, PACK * PAIRS :].bitcast(BF16).rearrange("p (c j) -> p c j", j=PACK)]
-        wv_grp.extend(held("wv_grp%d" % u, [P, WV_COLS, PACK], BF16)[:] for u in range(1, N // WV_COLS))
+        wv_grp.append(held("wv_grp1", [P, WV_COLS, PACK], BF16)[:])
+        wv_grp.append(shared[:, 0:PAIRS].bitcast(BF16).rearrange("p (c j) -> p c j", j=PACK))
         wv_codes = held("wv_codes", [P, N], U32)
         wv_sc = held("wv_sc", [P, N], U8)
 
@@ -321,17 +322,17 @@ def tile_list_ad_auction_bids_kernel(tc, tab_words, tab_scales, offs, w1, pos1, 
         cast_wv("g", 0, 0, 240)
         cast_wv("g", 1, 0, 240)
         cast_wv("s", 0, 240, WV_COLS)
-        sigmoid_rest(1, 3)
+        sigmoid_rest(2, 4)
         cast_wv("s", 1, 240, WV_COLS)
-        sigmoid_rest(3, 4)
-        sigmoid_rest(0, 1)
-        cast_wv("s", 2)
+        sigmoid_rest(0, 2)
+        cast_wv("s", 2, 0, 144)
         for t in range(PACK):
             gather_ad(t, starts[0], starts[0] + CHUNKS[0])
         cast_z("v", 0, 0, 256)
         quant_z(0)
         quant_wv(0)
         quant_wv(1)
+        cast_wv("v", 2, 144, WV_COLS)
         s2mm("val", 0, 0, 2)
         s2mm("clk", 0, 0, 2)
         s2mm("val", 0, 2, 4)

@@ -26,6 +26,7 @@ CHUNKS = [256, 256]
 WV_COLS = 256
 FIRST = 256
 HALF = 256
+LEAD = 96
 Z16TAG = ["za", "zb", "zc", "zd"]
 
 
@@ -124,7 +125,8 @@ def tile_list_ad_auction_bids_kernel(tc, tab_words, tab_scales, offs, w1, pos1, 
             load_wc_sc(q)
 
         grouped, w1_codes, w1_sc = {}, {}, {}
-        shared = held("shared", [P, (PACK + 1) * PAIRS], F32)
+        whole = held("shared", [P, LEAD + (PACK + 1) * PAIRS], F32)
+        shared = whole[:, LEAD:]
         picked = shared[:, 0 : PACK * PAIRS].rearrange("p (t j) -> p t j", t=PACK)
         late = shared[:, PAIRS:].bitcast(BF16).rearrange("p (t x) -> p t x", t=PACK)[:, :, 0:KP]
         for half in (CTX, AD):
@@ -201,15 +203,15 @@ def tile_list_ad_auction_bids_kernel(tc, tab_words, tab_scales, offs, w1, pos1, 
         def gather_ctx(t, j0, j1):
             nc.vector.tensor_copy(picked[:, slot(t), j0:j1], h[CTX, t][:].indirect(pos2_sb[:, j0 // 16 : j1 // 16]))
 
-        def sigmoid_first(t):
-            nc.scalar.activation(gate[:, slot(t), 0:FIRST], picked[:, slot(t), 0:FIRST], ACT.Sigmoid)
+        def sigmoid_first(s0, s1):
+            nc.scalar.activation(gate[:, s0:s1, 0:FIRST], picked[:, s0:s1, 0:FIRST], ACT.Sigmoid)
 
         def sigmoid_rest(s0, s1):
             nc.scalar.activation(gate[:, s0:s1, FIRST:], picked[:, s0:s1, FIRST:], ACT.Sigmoid)
 
         wv_grp = [shared[:, PACK * PAIRS :].bitcast(BF16).rearrange("p (c j) -> p c j", j=PACK)]
         wv_grp.append(held("wv_grp1", [P, WV_COLS, PACK], BF16)[:])
-        wv_grp.append(shared[:, 0:PAIRS].bitcast(BF16).rearrange("p (c j) -> p c j", j=PACK))
+        wv_grp.append(whole[:, 0:PAIRS].bitcast(BF16).rearrange("p (c j) -> p c j", j=PACK))
         wv_codes = held("wv_codes", [P, N], U32)
         wv_sc = held("wv_sc", [P, N], U8)
 
@@ -298,7 +300,8 @@ def tile_list_ad_auction_bids_kernel(tc, tab_words, tab_scales, offs, w1, pos1, 
         gather_tab(1, 0, S)
         cast_w1t("v", CTX, 1, 0, 2)
         cast_w1t("s", CTX, 1, 2, 4)
-        quant_w1t(CTX, 1, 0, 2)
+        quant_w1t(CTX, 1, 0, 1)
+        quant_w1t(CTX, 1, 1, 2)
         quant_w1t(CTX, 1, 2, 4)
         for t in range(PACK):
             for ih in range(2):
@@ -307,32 +310,37 @@ def tile_list_ad_auction_bids_kernel(tc, tab_words, tab_scales, offs, w1, pos1, 
         cast_w1t("v", AD, 0, 0, 4)
         quant_w1t(AD, 0, 0, 4)
         cast_w1t("v", AD, 1, 0, 4, 0, 64)
-        cast_w1t("v", AD, 1, 0, 4, 64, 128)
+        cast_w1t("v", AD, 1, 0, 2, 64, 128)
+        cast_w1t("v", AD, 1, 2, 4, 64, 128)
         for t in range(PACK):
             quant_w1t(AD, 1, t, t + 1)
         for t in range(PACK):
             gather_ctx(t, 0, PAIRS)
         for t in range(PACK):
             for ih in range(2):
-                first = 0 if t < 2 else 1
+                first = 0 if t < 1 else 1
                 mm1(AD, t, ih, first, first)
                 mm1(AD, t, ih, 1 - first, first)
                 h_out("s", AD, t, ih)
-            sigmoid_first(t)
+            if t == 1:
+                sigmoid_first(1, 3)
+            if t == 2:
+                sigmoid_first(3, 4)
+        sigmoid_first(0, 1)
         cast_wv("g", 0, 0, 240)
         cast_wv("g", 1, 0, 240)
         cast_wv("s", 0, 240, WV_COLS)
         sigmoid_rest(2, 4)
         cast_wv("s", 1, 240, WV_COLS)
         sigmoid_rest(0, 2)
-        cast_wv("s", 2, 0, 144)
+        cast_wv("s", 2, 0, 176)
         for t in range(PACK):
             gather_ad(t, starts[0], starts[0] + CHUNKS[0])
         cast_z("v", 0, 0, 256)
         quant_z(0)
         quant_wv(0)
         quant_wv(1)
-        cast_wv("v", 2, 144, WV_COLS)
+        cast_wv("v", 2, 176, WV_COLS)
         s2mm("val", 0, 0, 2)
         s2mm("clk", 0, 0, 2)
         s2mm("val", 0, 2, 4)

@@ -26,7 +26,7 @@ CHUNKS = [256, 256]
 WV_COLS = 256
 FIRST = 256
 HALF = 256
-LEAD = 96
+LEAD = 0
 Z16TAG = ["za", "zb", "zc", "zd"]
 
 
@@ -115,9 +115,9 @@ def tile_list_ad_auction_bids_kernel(tc, tab_words, tab_scales, offs, w1, pos1, 
         load_w1(AD, 0, 0, H)
         load_w1(AD, 1, 0, H // 2)
         load_w1(AD, 1, H // 2, H)
-        load_list("pos1")
-        load_wv(0)
         load_list("pos2")
+        load_wv(0)
+        load_list("pos1")
         load_wv(1)
         load_wv(2)
         load_wc()
@@ -327,20 +327,20 @@ def tile_list_ad_auction_bids_kernel(tc, tab_words, tab_scales, offs, w1, pos1, 
             if t == 2:
                 sigmoid_first(3, 4)
         sigmoid_first(0, 1)
-        cast_wv("g", 0, 0, 240)
-        cast_wv("g", 1, 0, 240)
-        cast_wv("s", 0, 240, WV_COLS)
+        cast_wv("g", 0, 0, 216)
+        cast_wv("g", 1, 0, 216)
+        cast_wv("s", 0, 216, WV_COLS)
         sigmoid_rest(2, 4)
-        cast_wv("s", 1, 240, WV_COLS)
+        cast_wv("s", 1, 216, WV_COLS)
         sigmoid_rest(0, 2)
-        cast_wv("s", 2, 0, 176)
+        cast_wv("s", 2, 0, 128)
         for t in range(PACK):
             gather_ad(t, starts[0], starts[0] + CHUNKS[0])
         cast_z("v", 0, 0, 256)
         quant_z(0)
         quant_wv(0)
         quant_wv(1)
-        cast_wv("v", 2, 176, WV_COLS)
+        cast_wv("v", 2, 128, WV_COLS)
         s2mm("val", 0, 0, 2)
         s2mm("clk", 0, 0, 2)
         s2mm("val", 0, 2, 4)

@@ -327,11 +327,11 @@ def tile_list_ad_auction_bids_kernel(tc, tab_words, tab_scales, offs, w1, pos1, 
             if t == 2:
                 sigmoid_first(3, 4)
         sigmoid_first(0, 1)
-        cast_wv("g", 0, 0, 216)
-        cast_wv("g", 1, 0, 216)
-        cast_wv("s", 0, 216, WV_COLS)
+        cast_wv("g", 0, 0, 248)
+        cast_wv("g", 1, 0, 248)
+        cast_wv("s", 0, 248, WV_COLS)
         sigmoid_rest(2, 4)
-        cast_wv("s", 1, 216, WV_COLS)
+        cast_wv("s", 1, 248, WV_COLS)
         sigmoid_rest(0, 2)
         cast_wv("s", 2, 0, 128)
         for t in range(PACK):

@@ -26,7 +26,7 @@ CHUNKS = [256, 256]
 WV_COLS = 256
 FIRST = 256
 HALF = 256
-LEAD = 0
+LEAD = 128
 Z16TAG = ["za", "zb", "zc", "zd"]
 
 
@@ -333,14 +333,14 @@ def tile_list_ad_auction_bids_kernel(tc, tab_words, tab_scales, offs, w1, pos1, 
         sigmoid_rest(2, 4)
         cast_wv("s", 1, 248, WV_COLS)
         sigmoid_rest(0, 2)
-        cast_wv("s", 2, 0, 128)
+        cast_wv("s", 2, 0, 192)
         for t in range(PACK):
             gather_ad(t, starts[0], starts[0] + CHUNKS[0])
         cast_z("v", 0, 0, 256)
         quant_z(0)
         quant_wv(0)
         quant_wv(1)
-        cast_wv("v", 2, 128, WV_COLS)
+        cast_wv("v", 2, 192, WV_COLS)
         s2mm("val", 0, 0, 2)
         s2mm("clk", 0, 0, 2)
         s2mm("val", 0, 2, 4)
@@ -368,5 +368,7 @@ def tile_list_ad_auction_bids_kernel(tc, tab_words, tab_scales, offs, w1, pos1, 
         s2mm("clk", 1, 4, 5)
         ms(4, 5, 256, 512)
         s2mm("val", 1, 5, 6)
-        s2mm("clk", 1, 5, 6)
-        ms(5, 6, 256, 512)
+        s2mm("clk", 1, 5, 6, 0, 128)
+        ms(5, 6, 256, 384)
+        s2mm("clk", 1, 5, 6, 128, 256)
+        ms(5, 6, 384, 512)

@@ -27,6 +27,9 @@ WV_COLS = 256
 FIRST = 256
 HALF = 256
 LEAD = 128
+LATE = 272
+GB, SC, OPEN = 176, 112, 1
+HALVED = ((CTX, 1), (AD, 0), (AD, 1))
 Z16TAG = ["za", "zb", "zc", "zd"]
 
 
@@ -57,15 +60,15 @@ def tile_list_ad_auction_bids_kernel(tc, tab_words, tab_scales, offs, w1, pos1, 
         raw = {}
         for half in (CTX, AD):
             for a in range(2):
-                if (half, a) != (AD, 1):
+                if (half, a) not in HALVED:
                     raw[half, a] = held("raw%d%d" % (half, a), [P, PACK, H], F32)
-        last_raw = [held("last_raw%d" % u, [P, PACK, H // 2], F32) for u in range(2)]
+        piece = {(half, a, u): held("piece%d%d%d" % (half, a, u), [P, PACK, H // 2], F32) for half, a in HALVED for u in range(2)}
         wv_raw = [held("wv_raw%d" % u, [P, PACK, WV_COLS], F32) for u in range(N // WV_COLS)]
         wc_codes = held("wc_codes", [P, 2 * N], U8)
 
         def load_w1(half, a, c0, c1):
             rows = w1[KP * a : KP * (a + 1), half * H + c0 : half * H + c1]
-            dst = last_raw[c0 // (H // 2)][:] if (half, a) == (AD, 1) else raw[half, a][:, :, c0:c1]
+            dst = piece[half, a, c0 // (H // 2)][:] if (half, a) in HALVED else raw[half, a][:, :, c0:c1]
             nc.sync.dma_start(out=dst, in_=rows.rearrange("(p j) c -> p j c", j=PACK))
 
         def load_tab(a):
@@ -111,11 +114,13 @@ def tile_list_ad_auction_bids_kernel(tc, tab_words, tab_scales, offs, w1, pos1, 
         load_tab(1)
         for r in range(4):
             move_sc(1, r)
-        load_w1(CTX, 1, 0, H)
-        load_w1(AD, 0, 0, H)
+        load_w1(CTX, 1, 0, H // 2)
+        load_w1(CTX, 1, H // 2, H)
+        load_w1(AD, 0, 0, H // 2)
+        load_w1(AD, 0, H // 2, H)
+        load_list("pos2")
         load_w1(AD, 1, 0, H // 2)
         load_w1(AD, 1, H // 2, H)
-        load_list("pos2")
         load_wv(0)
         load_list("pos1")
         load_wv(1)
@@ -128,7 +133,7 @@ def tile_list_ad_auction_bids_kernel(tc, tab_words, tab_scales, offs, w1, pos1, 
         whole = held("shared", [P, LEAD + (PACK + 1) * PAIRS], F32)
         shared = whole[:, LEAD:]
         picked = shared[:, 0 : PACK * PAIRS].rearrange("p (t j) -> p t j", t=PACK)
-        late = shared[:, PAIRS:].bitcast(BF16).rearrange("p (t x) -> p t x", t=PACK)[:, :, 0:KP]
+        late = shared[:, LATE : LATE + PACK * PAIRS].bitcast(BF16).rearrange("p (t x) -> p t x", t=PACK)[:, :, 0:KP]
         for half in (CTX, AD):
             for a in range(2):
                 if (half, a) != (AD, 1):
@@ -149,7 +154,7 @@ def tile_list_ad_auction_bids_kernel(tc, tab_words, tab_scales, offs, w1, pos1, 
                 dst = late[:, t0:t1, :].rearrange("p t (m j) -> p m j t", j=PACK)
             else:
                 dst = grouped[half, a][:, KP * t0 : KP * t1].rearrange("p (t m j) -> p m j t", m=P, j=PACK)
-            rows = last_raw[m0 // (P // 2)] if (half, a) == (AD, 1) else raw[half, a]
+            rows = piece[half, a, m0 // (P // 2)] if (half, a) in HALVED else raw[half, a]
             src = rows[:].rearrange("p j (m t) -> p m j t", t=PACK)[:, :, :, t0:t1]
             cast(eng, dst[:, m0:m1], src)
 
@@ -198,10 +203,15 @@ def tile_list_ad_auction_bids_kernel(tc, tab_words, tab_scales, offs, w1, pos1, 
         gate = gate_row[:].rearrange("p (t j) -> p t j", t=PACK)
 
         def slot(t):
-            return (t + 1) % PACK
+            return (t - 1) % PACK
+
+        early = piece[AD, 1, 0][:, 0, :]
+
+        def sigmoid_early():
+            nc.scalar.activation(gate[:, slot(0), 0:FIRST], early, ACT.Sigmoid)
 
         def gather_ctx(t, j0, j1):
-            nc.vector.tensor_copy(picked[:, slot(t), j0:j1], h[CTX, t][:].indirect(pos2_sb[:, j0 // 16 : j1 // 16]))
+            nc.vector.tensor_copy(early if (t, j0) == (0, 0) else picked[:, slot(t), j0:j1], h[CTX, t][:].indirect(pos2_sb[:, j0 // 16 : j1 // 16]))
 
         def sigmoid_first(s0, s1):
             nc.scalar.activation(gate[:, s0:s1, 0:FIRST], picked[:, s0:s1, 0:FIRST], ACT.Sigmoid)
@@ -298,8 +308,9 @@ def tile_list_ad_auction_bids_kernel(tc, tab_words, tab_scales, offs, w1, pos1, 
             for ih in range(2):
                 mm1(CTX, t, ih, 0)
         gather_tab(1, 0, S)
-        cast_w1t("v", CTX, 1, 0, 2)
-        cast_w1t("s", CTX, 1, 2, 4)
+        cast_w1t("s", CTX, 1, 0, 4, 0, 64)
+        cast_w1t("v", CTX, 1, 0, 2, 64, 128)
+        cast_w1t("v", CTX, 1, 2, 4, 64, 128)
         quant_w1t(CTX, 1, 0, 1)
         quant_w1t(CTX, 1, 1, 2)
         quant_w1t(CTX, 1, 2, 4)
@@ -307,40 +318,44 @@ def tile_list_ad_auction_bids_kernel(tc, tab_words, tab_scales, offs, w1, pos1, 
             for ih in range(2):
                 mm1(CTX, t, ih, 1)
                 h_out("s", CTX, t, ih)
-        cast_w1t("v", AD, 0, 0, 4)
-        quant_w1t(AD, 0, 0, 4)
+        cast_w1t("v", AD, 0, 0, 4, 0, 64)
+        cast_w1t("v", AD, 0, 0, 2, 64, 128)
+        cast_w1t("v", AD, 0, 2, 4, 64, 128)
+        quant_w1t(AD, 0, 0, 2)
+        quant_w1t(AD, 0, 2, 4)
         cast_w1t("v", AD, 1, 0, 4, 0, 64)
+        gather_ctx(0, 0, FIRST)
+        sigmoid_early()
         cast_w1t("v", AD, 1, 0, 2, 64, 128)
         cast_w1t("v", AD, 1, 2, 4, 64, 128)
         for t in range(PACK):
             quant_w1t(AD, 1, t, t + 1)
-        for t in range(PACK):
+        for t in range(1, PACK):
             gather_ctx(t, 0, PAIRS)
+        gather_ctx(0, FIRST, PAIRS)
         for t in range(PACK):
             for ih in range(2):
-                first = 0 if t < 1 else 1
+                first = 0 if t < OPEN else 1
                 mm1(AD, t, ih, first, first)
                 mm1(AD, t, ih, 1 - first, first)
                 h_out("s", AD, t, ih)
             if t == 1:
-                sigmoid_first(1, 3)
+                sigmoid_first(0, 2)
             if t == 2:
-                sigmoid_first(3, 4)
-        sigmoid_first(0, 1)
-        cast_wv("g", 0, 0, 248)
-        cast_wv("g", 1, 0, 248)
-        cast_wv("s", 0, 248, WV_COLS)
-        sigmoid_rest(2, 4)
-        cast_wv("s", 1, 248, WV_COLS)
+                sigmoid_first(2, 3)
+        cast_wv("g", 0, 0, WV_COLS)
+        cast_wv("g", 1, 0, GB)
+        cast_wv("s", 1, GB, WV_COLS)
         sigmoid_rest(0, 2)
-        cast_wv("s", 2, 0, 192)
+        sigmoid_rest(2, 4)
+        cast_wv("s", 2, 0, SC)
         for t in range(PACK):
             gather_ad(t, starts[0], starts[0] + CHUNKS[0])
         cast_z("v", 0, 0, 256)
         quant_z(0)
         quant_wv(0)
         quant_wv(1)
-        cast_wv("v", 2, 192, WV_COLS)
+        cast_wv("v", 2, SC, WV_COLS)
         s2mm("val", 0, 0, 2)
         s2mm("clk", 0, 0, 2)
         s2mm("val", 0, 2, 4)

@@ -27,8 +27,9 @@ WV_COLS = 256
 FIRST = 256
 HALF = 256
 LEAD = 128
-LATE = 272
-GB, SC, OPEN = 176, 112, 1
+LATE = 16
+LATE_STEP = 768
+GB, SC, OPEN = 168, 128, 2
 HALVED = ((CTX, 1), (AD, 0), (AD, 1))
 Z16TAG = ["za", "zb", "zc", "zd"]
 
@@ -130,10 +131,10 @@ def tile_list_ad_auction_bids_kernel(tc, tab_words, tab_scales, offs, w1, pos1, 
             load_wc_sc(q)
 
         grouped, w1_codes, w1_sc = {}, {}, {}
-        whole = held("shared", [P, LEAD + (PACK + 1) * PAIRS], F32)
+        whole = held("shared", [P, LEAD + LATE + PACK * LATE_STEP], F32)
         shared = whole[:, LEAD:]
         picked = shared[:, 0 : PACK * PAIRS].rearrange("p (t j) -> p t j", t=PACK)
-        late = shared[:, LATE : LATE + PACK * PAIRS].bitcast(BF16).rearrange("p (t x) -> p t x", t=PACK)[:, :, 0:KP]
+        late = shared[:, LATE : LATE + PACK * LATE_STEP].bitcast(BF16).rearrange("p (t x) -> p t x", t=PACK)[:, :, 0:KP]
         for half in (CTX, AD):
             for a in range(2):
                 if (half, a) != (AD, 1):
@@ -205,7 +206,7 @@ def tile_list_ad_auction_bids_kernel(tc, tab_words, tab_scales, offs, w1, pos1, 
         def slot(t):
             return (t - 1) % PACK
 
-        early = piece[AD, 1, 0][:, 0, :]
+        early = grouped[AD, 0].bitcast(F32)[:, 0:FIRST]
 
         def sigmoid_early():
             nc.scalar.activation(gate[:, slot(0), 0:FIRST], early, ACT.Sigmoid)
@@ -219,8 +220,7 @@ def tile_list_ad_auction_bids_kernel(tc, tab_words, tab_scales, offs, w1, pos1, 
         def sigmoid_rest(s0, s1):
             nc.scalar.activation(gate[:, s0:s1, FIRST:], picked[:, s0:s1, FIRST:], ACT.Sigmoid)
 
-        wv_grp = [shared[:, PACK * PAIRS :].bitcast(BF16).rearrange("p (c j) -> p c j", j=PACK)]
-        wv_grp.append(held("wv_grp1", [P, WV_COLS, PACK], BF16)[:])
+        wv_grp = [shared[:, (PACK + u) * PAIRS : (PACK + u + 1) * PAIRS].bitcast(BF16).rearrange("p (c j) -> p c j", j=PACK) for u in range(2)]
         wv_grp.append(whole[:, 0:PAIRS].bitcast(BF16).rearrange("p (c j) -> p c j", j=PACK))
         wv_codes = held("wv_codes", [P, N], U32)
         wv_sc = held("wv_sc", [P, N], U8)
@@ -373,8 +373,9 @@ def tile_list_ad_auction_bids_kernel(tc, tab_words, tab_scales, offs, w1, pos1, 
         ms(2, 4, 0, 256)
         ms(4, 6, 0, 256)
         s2mm("val", 1, 0, 2, 0, 128)
+        s2mm("clk", 1, 0, 2, 0, 128)
         s2mm("val", 1, 0, 2, 128, 256)
-        s2mm("clk", 1, 0, 2)
+        s2mm("clk", 1, 0, 2, 128, 256)
         ms(0, 2, 256, 512)
         s2mm("val", 1, 2, 4)
         s2mm("clk", 1, 2, 4)

@@ -27,6 +27,7 @@ WV_COLS = 256
 FIRST = 256
 HALF = 256
 LEAD = 128
+OPEN_CTX = 2
 LATE = 16
 LATE_STEP = 768
 GB, SC, OPEN = 168, 128, 2
@@ -304,7 +305,7 @@ def tile_list_ad_auction_bids_kernel(tc, tab_words, tab_scales, offs, w1, pos1, 
         cast_w1t("s", CTX, 0, 0, 4)
         quant_w1t(CTX, 0, 0, 4)
         gather_tab(0, 0, S)
-        for t in range(PACK):
+        for t in range(OPEN_CTX):
             for ih in range(2):
                 mm1(CTX, t, ih, 0)
         gather_tab(1, 0, S)
@@ -316,7 +317,11 @@ def tile_list_ad_auction_bids_kernel(tc, tab_words, tab_scales, offs, w1, pos1, 
         quant_w1t(CTX, 1, 2, 4)
         for t in range(PACK):
             for ih in range(2):
-                mm1(CTX, t, ih, 1)
+                if t < OPEN_CTX:
+                    mm1(CTX, t, ih, 1)
+                else:
+                    mm1(CTX, t, ih, 1, 1)
+                    mm1(CTX, t, ih, 0, 1)
                 h_out("s", CTX, t, ih)
         cast_w1t("v", AD, 0, 0, 4, 0, 64)
         cast_w1t("v", AD, 0, 0, 2, 64, 128)

@@ -344,11 +344,13 @@ def tile_list_ad_auction_bids_kernel(tc, tab_words, tab_scales, offs, w1, pos1, 
                 mm1(AD, t, ih, first, first)
                 mm1(AD, t, ih, 1 - first, first)
                 h_out("s", AD, t, ih)
+                if (t, ih) == (3, 0):
+                    cast_wv("s", 0, 248, WV_COLS)
             if t == 1:
                 sigmoid_first(0, 2)
             if t == 2:
                 sigmoid_first(2, 3)
-        cast_wv("g", 0, 0, WV_COLS)
+        cast_wv("g", 0, 0, 248)
         cast_wv("g", 1, 0, GB)
         cast_wv("s", 1, GB, WV_COLS)
         sigmoid_rest(0, 2)
@@ -378,9 +380,8 @@ def tile_list_ad_auction_bids_kernel(tc, tab_words, tab_scales, offs, w1, pos1, 
         ms(2, 4, 0, 256)
         ms(4, 6, 0, 256)
         s2mm("val", 1, 0, 2, 0, 128)
-        s2mm("clk", 1, 0, 2, 0, 128)
         s2mm("val", 1, 0, 2, 128, 256)
-        s2mm("clk", 1, 0, 2, 128, 256)
+        s2mm("clk", 1, 0, 2)
         ms(0, 2, 256, 512)
         s2mm("val", 1, 2, 4)
         s2mm("clk", 1, 2, 4)

from contextlib import ExitStack

import concourse.mybir as mybir

K, T, S, PAIRS, H, G, N = 1024, 4096, 1024, 512, 512, 1024, 768
FLOPS = 2 * K * G * S + 4 * H * N * PAIRS

F32 = mybir.dt.float32
BF16 = mybir.dt.bfloat16
I32 = mybir.dt.int32
U32 = mybir.dt.uint32
U16 = mybir.dt.uint16
U8 = mybir.dt.uint8
FP8X4 = mybir.dt.float8_e4m3fn_x4
FP4X4 = mybir.dt.float4_e2m1fn_x4
ACT = mybir.ActivationFunctionType
ALU = mybir.AluOpType

P = 128
PACK = 4
KP = 512
BANK = 512
LN_HALF = -0.6931471805599453
CTX, AD = 1, 0
CHUNKS = [256, 256]
WV_COLS = 256
FIRST = 256
HALF = 256
LEAD = 128
OPEN_CTX = 2
LATE = 16
LATE_STEP = 768
GB, SC, OPEN = 168, 128, 2
HALVED = ((CTX, 1), (AD, 0), (AD, 1))
Z16TAG = ["za", "zb", "zc", "zd"]


def tile_list_ad_auction_bids_kernel(tc, tab_words, tab_scales, offs, w1, pos1, pos2, wc_words, wc_scales, wv, out):
    nc = tc.nc
    with ExitStack() as ctx:
        keep = ctx.enter_context(tc.tile_pool(name="keep", bufs=1))
        psum = ctx.enter_context(tc.psum_pool(name="psum", bufs=8))

        def held(name, shape, dtype, tag=None):
            return keep.tile(shape, dtype, name=name, tag=tag or name, align_bytes=64)

        offs_sb = keep.tile([P, S // 16], U16, name="offs_sb")
        pos1_sb = keep.tile([P, PAIRS // 16], U16, name="pos1_sb")
        pos2_sb = keep.tile([P, PAIRS // 16], U16, name="pos2_sb")

        tab_sc = held("tab_sc", [P, T // 4], I32)
        wc_sc = held("wc_sc", [P, N // 4], I32)
        nc.vector.memset(tab_sc[:], 0)
        planes = held("planes", [P, S // 4], I32)
        nc.vector.memset(planes[:], 0)
        nc.vector.memset(wc_sc[:], 0)
        warm = held("warm", [P, 16], F32)
        nc.vector.memset(warm[:, 0:8], 0.0)
        nc.scalar.activation(warm[:, 8:16], warm[:, 0:8], ACT.Sigmoid)

        tab = [held("tab%d" % a, [P, T], I32) for a in range(2)]
        raw = {}
        for half in (CTX, AD):
            for a in range(2):
                if (half, a) not in HALVED:
                    raw[half, a] = held("raw%d%d" % (half, a), [P, PACK, H], F32)
        piece = {(half, a, u): held("piece%d%d%d" % (half, a, u), [P, PACK, H // 2], F32) for half, a in HALVED for u in range(2)}
        wv_raw = [held("wv_raw%d" % u, [P, PACK, WV_COLS], F32) for u in range(N // WV_COLS)]
        wc_codes = held("wc_codes", [P, 2 * N], U8)

        def load_w1(half, a, c0, c1):
            rows = w1[KP * a : KP * (a + 1), half * H + c0 : half * H + c1]
            dst = piece[half, a, c0 // (H // 2)][:] if (half, a) in HALVED else raw[half, a][:, :, c0:c1]
            nc.sync.dma_start(out=dst, in_=rows.rearrange("(p j) c -> p j c", j=PACK))

        def load_tab(a):
            nc.sync.dma_start(out=tab[a][:], in_=tab_words[a].rearrange("p n t -> p (n t)").bitcast(I32))

        ts32 = tab_scales.bitcast(I32)
        ws32 = wc_scales.bitcast(I32)

        def load_tab_sc():
            nc.sync.dma_start(out=tab_sc[0:P:4, :], in_=ts32.rearrange("a q t -> (a q) t"))

        def load_wc_sc(q):
            nc.sync.dma_start(out=wc_sc[32 * q : 32 * q + 4, :], in_=ws32[0, 4 * q : 4 * q + 4, :])

        got_sc = held("got_sc", [P, S], U8)

        def gather_sc():
            nc.vector.tensor_copy(got_sc[:], tab_sc[:].bitcast(U8).indirect(offs_sb[:]))

        def move_sc(a, r):
            nc.sync.dma_start(out=planes[4 * a + r : P : 32, :], in_=got_sc[:].bitcast(I32)[64 * a + 4 * r : 64 * (a + 1) : 16, :])

        lists = {"offs": (offs_sb, offs), "pos1": (pos1_sb, pos1), "pos2": (pos2_sb, pos2)}

        def load_list(name):
            nc.sync.dma_start(lists[name][0][:], lists[name][1])

        def load_wv(u):
            nc.sync.dma_start(out=wv_raw[u][:], in_=wv[:, WV_COLS * u : WV_COLS * (u + 1)].rearrange("(p j) c -> p j c", j=PACK))

        def load_wc():
            nc.sync.dma_start(out=wc_codes[:].bitcast(I32), in_=wc_words[0].bitcast(I32))

        rows0 = w1[0:KP, CTX * H : (CTX + 1) * H].rearrange("(p j) c -> p j c", j=PACK)
        nc.sync.dma_start(out=raw[CTX, 0][:, 0:2, :], in_=rows0[:, 0:2, :])
        load_list("offs")
        load_tab_sc()
        nc.sync.dma_start(out=raw[CTX, 0][:, 2:4, :], in_=rows0[:, 2:4, :])
        load_tab(0)
        gather_sc()
        for r in range(4):
            move_sc(0, r)
        load_tab(1)
        for r in range(4):
            move_sc(1, r)
        load_w1(CTX, 1, 0, H // 2)
        load_w1(CTX, 1, H // 2, H)
        load_w1(AD, 0, 0, H // 2)
        load_w1(AD, 0, H // 2, H)
        load_list("pos2")
        load_w1(AD, 1, 0, H // 2)
        load_w1(AD, 1, H // 2, H)
        load_wv(0)
        load_list("pos1")
        load_wv(1)
        load_wv(2)
        load_wc()
        for q in range(4):
            load_wc_sc(q)

        grouped, w1_codes, w1_sc = {}, {}, {}
        whole = held("shared", [P, LEAD + LATE + PACK * LATE_STEP], F32)
        shared = whole[:, LEAD:]
        picked = shared[:, 0 : PACK * PAIRS].rearrange("p (t j) -> p t j", t=PACK)
        late = shared[:, LATE : LATE + PACK * LATE_STEP].bitcast(BF16).rearrange("p (t x) -> p t x", t=PACK)[:, :, 0:KP]
        for half in (CTX, AD):
            for a in range(2):
                if (half, a) != (AD, 1):
                    grouped[half, a] = held("grp%d%d" % (half, a), [P, PACK * H], BF16)[:]
                w1_codes[half, a] = held("w1c%d%d" % (half, a), [P, H], U32)
                w1_sc[half, a] = held("w1s%d%d" % (half, a), [P, H], U8)

        def cast(eng, dst, src):
            if eng == "v":
                nc.vector.tensor_copy(out=dst, in_=src)
            elif eng == "s":
                nc.scalar.copy(out=dst, in_=src)
            else:
                nc.gpsimd.tensor_scalar(dst, src, 1.0, 0.0, ALU.mult, ALU.add)

        def cast_w1t(eng, half, a, t0, t1, m0=0, m1=P):
            if (half, a) == (AD, 1):
                dst = late[:, t0:t1, :].rearrange("p t (m j) -> p m j t", j=PACK)
            else:
                dst = grouped[half, a][:, KP * t0 : KP * t1].rearrange("p (t m j) -> p m j t", m=P, j=PACK)
            rows = piece[half, a, m0 // (P // 2)] if (half, a) in HALVED else raw[half, a]
            src = rows[:].rearrange("p j (m t) -> p m j t", t=PACK)[:, :, :, t0:t1]
            cast(eng, dst[:, m0:m1], src)

        def quant_w1t(half, a, t0, t1):
            nc.vector.quantize_mx(
                out=w1_codes[half, a][:, P * t0 : P * t1].bitcast(FP8X4),
                scales=w1_sc[half, a][:, P * t0 : P * t1],
                in_=late[:, t0, :] if (half, a) == (AD, 1) else grouped[half, a][:, KP * t0 : KP * t1],
            )

        got = [held("got%d" % a, [P, S], U32) for a in range(2)]

        def gather_tab(a, i0, i1):
            nc.vector.tensor_copy(got[a][:, i0:i1], tab[a][:].bitcast(U32).indirect(offs_sb[:, i0 // 16 : i1 // 16]))


        acc = {}

        def mm1(half, t, ih, a, first=0):
            if a == first:
                acc[half, t, ih] = psum.tile([P, BANK], F32, name="bank")
            cols = slice(BANK * ih, BANK * (ih + 1))
            nc.tensor.matmul_mx(
                out=acc[half, t, ih][:],
                lhsT=w1_codes[half, a][:, P * t : P * (t + 1)].bitcast(FP8X4),
                lhsT_scale=w1_sc[half, a][:, P * t : P * (t + 1)],
                rhs=got[a][:, cols].bitcast(FP8X4),
                rhs_scale=planes[:].bitcast(U8)[4 * a : P, cols],
                start=(a == first),
                stop=(a != first),
            )

        h = {}
        for half in (CTX, AD):
            for t in range(PACK):
                h[half, t] = held("h%d%d" % (half, t), [P, S], F32)

        def h_out(eng, half, t, ih):
            dst = h[half, t][:, BANK * ih : BANK * (ih + 1)]
            if eng == "v":
                nc.vector.tensor_copy(out=dst, in_=acc[half, t, ih][:])
            else:
                nc.scalar.copy(out=dst, in_=acc[half, t, ih][:])

        gate_row = held("gate", [P, PACK * PAIRS], F32)
        gate = gate_row[:].rearrange("p (t j) -> p t j", t=PACK)

        def slot(t):
            return (t - 1) % PACK

        early = grouped[AD, 0].bitcast(F32)[:, 0:FIRST]

        def sigmoid_early():
            nc.scalar.activation(gate[:, slot(0), 0:FIRST], early, ACT.Sigmoid)

        def gather_ctx(t, j0, j1):
            nc.vector.tensor_copy(early if (t, j0) == (0, 0) else picked[:, slot(t), j0:j1], h[CTX, t][:].indirect(pos2_sb[:, j0 // 16 : j1 // 16]))

        def sigmoid_first(s0, s1):
            nc.scalar.activation(gate[:, s0:s1, 0:FIRST], picked[:, s0:s1, 0:FIRST], ACT.Sigmoid)

        def sigmoid_rest(s0, s1):
            nc.scalar.activation(gate[:, s0:s1, FIRST:], picked[:, s0:s1, FIRST:], ACT.Sigmoid)

        wv_grp = [shared[:, (PACK + u) * PAIRS : (PACK + u + 1) * PAIRS].bitcast(BF16).rearrange("p (c j) -> p c j", j=PACK) for u in range(2)]
        wv_grp.append(whole[:, 0:PAIRS].bitcast(BF16).rearrange("p (c j) -> p c j", j=PACK))
        wv_codes = held("wv_codes", [P, N], U32)
        wv_sc = held("wv_sc", [P, N], U8)

        def cast_wv(eng, u, c0=0, c1=WV_COLS):
            src = wv_raw[u][:, :, c0:c1]
            dst = wv_grp[u][:, c0:c1, :]
            if eng == "g":
                cast(eng, dst, src.rearrange("p j c -> p c j"))
            else:
                cast(eng, dst.rearrange("p (c i) j -> p c j i", i=4), src.rearrange("p j (c i) -> p c j i", i=4))

        def quant_wv(u):
            c0, c1 = WV_COLS * u, WV_COLS * (u + 1)
            nc.vector.quantize_mx(
                out=wv_codes[:, c0:c1].bitcast(FP8X4),
                scales=wv_sc[:, c0:c1],
                in_=wv_grp[u][:].rearrange("p c j -> p (c j)"),
            )

        starts = [sum(CHUNKS[:c]) for c in range(len(CHUNKS))]
        z32 = held("z32", [P, PACK, PAIRS], F32)
        z16 = [held("z16_%d" % c, [P, n, PACK], BF16, Z16TAG[c]) for c, n in enumerate(CHUNKS)]
        z_codes = [held("zc_%d" % c, [P, n], U32) for c, n in enumerate(CHUNKS)]
        z_sc = [held("zs_%d" % c, [P, n], U8) for c, n in enumerate(CHUNKS)]

        def gather_ad(t, j0, j1):
            nc.vector.tensor_tensor(
                z32[:, t, j0:j1], h[AD, t][:].indirect(pos1_sb[:, j0 // 16 : j1 // 16]), gate[:, slot(t), j0:j1], ALU.mult
            )

        def cast_z(eng, c, n0, n1):
            cast(eng, z16[c][:, n0:n1, :].rearrange("p (c i) j -> p c j i", i=4), z32[:, :, starts[c] + n0 : starts[c] + n1].rearrange("p j (c i) -> p c j i", i=4))

        def quant_z(c, n0=0, n1=HALF):
            nc.vector.quantize_mx(
                out=z_codes[c][:, n0:n1].bitcast(FP8X4), scales=z_sc[c][:, n0:n1], in_=z16[c][:, n0:n1, :].rearrange("p n t -> p (n t)")
            )

        wc_sc8 = wc_sc[:].bitcast(U8)

        act = {}
        bid = {}
        for g in range(2):
            for kind in ("val", "clk"):
                act[kind, g] = held("act_%s%d" % (kind, g), [P, N // P, HALF], F32)
            bid[g] = held("bid%d" % g, [P, N // P, HALF], F32)

        def s2mm(kind, c, n0, n1, j0=0, j1=HALF):
            bank = psum.tile([P, n1 - n0, j1 - j0], F32, name="bank")
            for m in range(n0, n1):
                cols = slice(P * m, P * (m + 1))
                if kind == "val":
                    codes, scales = wv_codes[:, cols].bitcast(FP8X4), wv_sc[:, cols]
                else:
                    codes, scales = wc_codes[:, 2 * cols.start : 2 * cols.stop].bitcast(FP4X4), wc_sc8[:, cols]
                nc.tensor.matmul_mx(
                    out=bank[:, m - n0, :], lhsT=codes, lhsT_scale=scales,
                    rhs=z_codes[c][:, j0:j1].bitcast(FP8X4), rhs_scale=z_sc[c][:, j0:j1], start=True, stop=True,
                )
            dst = act[kind, c][:, n0:n1, j0:j1]
            if kind == "val":
                nc.scalar.activation(dst, bank[:], ACT.Exp, bias=LN_HALF)
            else:
                nc.scalar.activation(dst, bank[:], ACT.Tanh, scale=0.5)

        def mul(n0, n1, j0, j1):
            g, o = divmod(j0, HALF)
            w = slice(o, o + j1 - j0)
            nc.vector.scalar_tensor_tensor(bid[g][:, n0:n1, w], act["clk", g][:, n0:n1, w], 1.0, act["val", g][:, n0:n1, w], ALU.add, ALU.mult)

        def store(n0, n1, j0, j1):
            g, o = divmod(j0, HALF)
            rows = out[P * n0 : P * n1, j0:j1]
            nc.sync.dma_start(out=rows.rearrange("(i p) c -> p i c", p=P), in_=bid[g][:, n0:n1, o : o + j1 - j0])

        def ms(n0, n1, j0, j1):
            mul(n0, n1, j0, j1)
            store(n0, n1, j0, j1)

        cast_w1t("s", CTX, 0, 0, 4)
        quant_w1t(CTX, 0, 0, 4)
        gather_tab(0, 0, S)
        for t in range(OPEN_CTX):
            for ih in range(2):
                mm1(CTX, t, ih, 0)
        gather_tab(1, 0, S)
        cast_w1t("s", CTX, 1, 0, 4, 0, 64)
        cast_w1t("v", CTX, 1, 0, 2, 64, 128)
        cast_w1t("v", CTX, 1, 2, 4, 64, 128)
        quant_w1t(CTX, 1, 0, 1)
        quant_w1t(CTX, 1, 1, 2)
        quant_w1t(CTX, 1, 2, 4)
        for t in range(PACK):
            for ih in range(2):
                if t < OPEN_CTX:
                    mm1(CTX, t, ih, 1)
                else:
                    mm1(CTX, t, ih, 1, 1)
                    mm1(CTX, t, ih, 0, 1)
                h_out("s", CTX, t, ih)
        cast_w1t("v", AD, 0, 0, 4, 0, 64)
        cast_w1t("v", AD, 0, 0, 2, 64, 128)
        cast_w1t("v", AD, 0, 2, 4, 64, 128)
        quant_w1t(AD, 0, 0, 2)
        quant_w1t(AD, 0, 2, 4)
        cast_w1t("v", AD, 1, 0, 4, 0, 64)
        gather_ctx(0, 0, FIRST)
        sigmoid_early()
        cast_w1t("v", AD, 1, 0, 2, 64, 128)
        cast_w1t("v", AD, 1, 2, 4, 64, 128)
        for t in range(PACK):
            quant_w1t(AD, 1, t, t + 1)
        for t in range(1, PACK):
            gather_ctx(t, 0, PAIRS)
        gather_ctx(0, FIRST, PAIRS)
        for t in range(PACK):
            for ih in range(2):
                first = 0 if t < OPEN else 1
                mm1(AD, t, ih, first, first)
                mm1(AD, t, ih, 1 - first, first)
                h_out("s", AD, t, ih)
                if (t, ih) == (3, 0):
                    cast_wv("s", 0, 248, WV_COLS)
            if t == 1:
                sigmoid_first(0, 2)
            if t == 2:
                sigmoid_first(2, 3)
        cast_wv("g", 0, 0, 248)
        cast_wv("g", 1, 0, GB)
        cast_wv("s", 1, GB, WV_COLS)
        sigmoid_rest(0, 2)
        sigmoid_rest(2, 4)
        cast_wv("s", 2, 0, SC)
        for t in range(PACK):
            gather_ad(t, starts[0], starts[0] + CHUNKS[0])
        cast_z("v", 0, 0, 256)
        quant_z(0)
        quant_wv(0)
        quant_wv(1)
        cast_wv("v", 2, SC, WV_COLS)
        s2mm("val", 0, 0, 2)
        s2mm("clk", 0, 0, 2)
        s2mm("val", 0, 2, 4)
        s2mm("clk", 0, 2, 4)
        for t in range(PACK):
            gather_ad(t, starts[1], starts[1] + CHUNKS[1])
        cast_z("v", 1, 0, 128)
        cast_z("v", 1, 128, 256)
        quant_z(1, 0, 128)
        quant_z(1, 128, 256)
        quant_wv(2)
        s2mm("clk", 0, 4, 6)
        s2mm("val", 0, 4, 6)
        ms(0, 2, 0, 256)
        ms(2, 4, 0, 256)
        ms(4, 6, 0, 256)
        s2mm("val", 1, 0, 2, 0, 128)
        s2mm("val", 1, 0, 2, 128, 256)
        s2mm("clk", 1, 0, 2)
        ms(0, 2, 256, 512)
        s2mm("val", 1, 2, 4)
        s2mm("clk", 1, 2, 4)
        ms(2, 4, 256, 512)
        s2mm("val", 1, 4, 5)
        s2mm("clk", 1, 4, 5)
        ms(4, 5, 256, 512)
        s2mm("val", 1, 5, 6)
        s2mm("clk", 1, 5, 6, 0, 128)
        ms(5, 6, 256, 384)
        s2mm("clk", 1, 5, 6, 128, 256)
        ms(5, 6, 384, 512)
